import numpy as np, ml_dtypes
CORES = [66,74,82,90,194,202,210,218]
N = 8
BF = ml_dtypes.bfloat16
def gentries(a):
    return np.ascontiguousarray(a.reshape(8, 16, -1).transpose(0, 2, 1)).reshape(8, -1)
def gtable(e):
    e = np.asarray(e); return np.ascontiguousarray(e.reshape(8, -1, 16).transpose(0, 2, 1)).reshape(128, -1).astype(np.int32)
A, S, G, M, W = 1024, 160, 3, 3, 2144
def tabs(e):
    return np.stack([gtable(v.reshape(8, -1)) for v in e])
def alleles(rng, ex):
    return np.minimum(np.floor(256 * rng.random((N, 128, 2 * A), dtype=np.float32) ** ex.astype(np.float32)), 255).astype(BF)
def rivals(rng):
    k = (N, 8, G, M, A)
    return np.where(rng.random(k) < 0.5, rng.integers(0, A, k), rng.integers(A, W, k))
def setup_inputs(rng):
    return {"haps": alleles(rng, np.exp2(2 * rng.random((N, 128, 1)) - 1)), "eff": rng.integers(0, 128, (N, 128, 1)).astype(np.float32).astype(BF),
            "dam": tabs(rng.integers(0, A, (N, 8, G, A))), "rival": tabs(rivals(rng)), "gift": tabs(rng.integers(0, A, (N, 8, G, N - 1, S)))}
def setup_inputs_ties(rng):
    d = setup_inputs(rng); e = rng.integers(0, 2, (N, 8, 16, 1))
    d["haps"] = (254 * rng.integers(0, 2, (1, 128, 1)) + rng.integers(0, 2, (N, 128, 2 * A))).astype(np.float32).astype(BF)
    for r in range(N): e[r, rng.permutation(8)[:3]] = 0
    d["eff"] = e.reshape(N, 128, 1).astype(np.float32).astype(BF)
    v = rivals(rng); v[:, :, :, 1] = np.where(rng.random((N, 8, G, A)) < 0.25, v[:, :, :, 0], v[:, :, :, 1])
    d["rival"] = tabs(v); return d
def edge(rng, e, places):
    return np.where(rng.random(e.shape) < 0.5, rng.choice(np.array(places), e.shape), e)
def setup_inputs_ends(rng):
    d = setup_inputs(rng); d["haps"][:, :, :2] = 255; d["haps"][:, :, 2 * A - 2:] = 0
    e = rng.integers(0, 128, (N, 8, 16, 1))
    for r in range(N): e[r, rng.permutation(8)[:4]] = 127
    d["eff"] = e.reshape(N, 128, 1).astype(np.float32).astype(BF)
    d["dam"] = tabs(edge(rng, rng.integers(0, A, (N, 8, G, A)), [0, A - 1])); d["gift"] = tabs(edge(rng, rng.integers(0, A, (N, 8, G, N - 1, S)), [0, A - 1]))
    d["rival"] = tabs(edge(rng, rivals(rng), [0, A - 1] + [A + S * k for k in range(N - 1)] + [A + S * k + S - 1 for k in range(N - 1)])); return d
def setup_inputs_one(rng):
    d = setup_inputs(rng); a = rng.integers(0, A, (N, 8, G, A)); a[:, :, 0] = rng.integers(0, A, (N, 8, 1))
    v = rivals(rng); v[:, :, :, 0] = rng.integers(0, W, (N, 8, G, 1))
    b = np.zeros((N, 8, G, N - 1, S), np.int64); b[:] = rng.integers(0, A, (N, 8, G, N - 1, 1))
    d["dam"] = tabs(a); d["rival"] = tabs(v); d["gift"] = tabs(b); return d
def setup_inputs_guests(rng):
    d = setup_inputs(rng)
    v = np.zeros((N, 8, G, M * A), np.int64); v[:] = np.arange(M * A) % (W - A); d["rival"] = tabs(A + rng.permuted(v, axis=-1))
    a = np.zeros((N, 8, G, A), np.int64); a[:] = np.arange(A); d["dam"] = tabs(rng.permuted(a, axis=-1))
    b = np.zeros((N, 8, G, N - 1, A), np.int64); b[:] = np.arange(A); d["gift"] = tabs(rng.permuted(b, axis=-1)[..., :S]); return d
def setup_inputs_spread(rng):
    d = setup_inputs(rng); d["haps"] = alleles(rng, np.exp2(8 * rng.random((N, 128, 1)) - 4))
    d["eff"] = np.floor(128 * rng.random((N, 128, 1)) ** 4).astype(np.float32).astype(BF)
    def u(m, *k): return np.minimum((m * rng.random(k) ** 3).astype(np.int64), m - 1)
    k = (N, 8, G, M, A)
    d["dam"] = tabs(A - 1 - u(A, N, 8, G, A)); d["gift"] = tabs(u(A, N, 8, G, N - 1, S))
    d["rival"] = tabs(np.where(rng.random(k) < 0.5, u(A, *k), W - 1 - u(W - A, *k))); return d
def check_inputs(d):
    bad = []
    h = d["haps"].astype(np.float32); e = d["eff"].astype(np.float32)
    if not ((h >= 0) & (h <= 255) & (h == np.floor(h))).all(): bad.append("haps: whole numbers from 0 to 255")
    if not ((e >= 0) & (e <= 127) & (e == np.floor(e))).all(): bad.append("eff: whole numbers from 0 to 127")
    for k, top in (("dam", A), ("rival", W), ("gift", A)):
        if not ((d[k] >= 0) & (d[k] < top)).all(): bad.append(k + ": range")
    return bad
def reference(haps, eff, dam, rival, gift):
    h = haps.astype(np.int32).reshape(N, 8, 16, A, 2); e = eff.astype(np.int32).reshape(N, 8, 16, 1)
    dl = np.stack([gentries(a) for a in dam]).reshape(N, 8, G, A)
    rl = np.stack([gentries(a) for a in rival]).reshape(N, 8, G, M, A)
    gl = np.stack([gentries(a) for a in gift]).reshape(N, 8, G, N - 1, S)
    i = np.arange(A); mk = np.arange(16)[:, None]
    for t in range(G):
        new = np.zeros_like(h)
        for r in range(N):
            parts = [h[r]]
            for d in range(N - 1):
                q = (r - 1 - d) % N
                parts.append(np.take_along_axis(h[q], gl[q, :, t, d][:, None, :, None], 2))
            w = np.concatenate(parts, 2)
            v = np.sum(e[r] * (w[..., 0] + w[..., 1]), axis=1)
            best = rl[r, :, t, 0]
            for m in range(1, M):
                c = rl[r, :, t, m]; vb = np.take_along_axis(v, best, 1); vc = np.take_along_axis(v, c, 1)
                best = np.where((vc > vb) | ((vc == vb) & (c > best)), c, best)
            for k, p in enumerate((dl[r, :, t], best)):
                x = (181 * p + 75 * i + 217 * t + 389 * k) & 1023
                s = (x >> 9)[:, None]; c = ((x >> 5) & 15)[:, None]
                side = np.where(mk < c, s, 1 - s)
                both = np.take_along_axis(w, p[:, None, :, None], 2)
                new[r, ..., k] = np.take_along_axis(both, side[..., None], 3)[..., 0]
        h = new
    return {"y": h.reshape(N, 128, 2 * A).astype(BF)}

@@ -1,0 +1,419 @@
+from concourse.bass import DstId, RemoteDMATransfer
+from concourse.mybir import AluOpType, ActivationFunctionType
+
+A, SG, G, W = 1024, 160, 3, 2144
+BF, F32, I32, U16 = "bfloat16", "float32", "int32", "uint16"
+SCRATCH = {}
+for _d, _l in ((BF, "hap:2048 iot:128 idn:128 nid:128 hid:128 ef:16 bm:144 tab:96 tie:96 gS:1120 gD:1120 R:3072 "
+                    "sgd0:1024 sgd1:1024 sgd2:1024 Sd:1024 Xd:1024 sgs:1024 Ss:1024 Xs:1024 "
+                    "S0:2144 S1:2144 S2:2144 D0:2144 D1:2144 D2:2144"),
+               (F32, "rs:576 u2:192 ta:192 tb:192 cid:192 cir:576 cols:8 jb:8 zz:96 za:96 kk:96 rst:96 M:96 nf:96 sel:192"),
+               (I32, "dl:192 rl:576 ti:192 tj:192 pc:8"),
+               (U16, "goff:210 doff:192 dz:192 roff:576 so:128")):
+    for _x in _l.split():
+        SCRATCH[_x.split(":")[0]] = ("sbuf", [128, int(_x.split(":")[1])], _d)
+SCRATCH["gl"] = ("sbuf", [128, 21, 10], I32)
+for _n in ("pv0", "pv1", "ps0", "ps1", "ps2", "ps3", "pd0", "pd1"):
+    SCRATCH[_n] = ("psum", [128, 512], F32)
+KEYS = ["%s%d" % (k, t) for t in range(G) for k in "SD"]
+SEMAPHORES = (["c_pe", "c_v", "c_a", "c_g", "l_h0", "l_h1", "l_gl", "l_dl", "l_ef", "l_r0", "l_r1", "st", "sentS", "sentD"]
+              + ["ar" + k for k in KEYS])
+
+CALLS = {k: [(3, 0, k[0] == "S"), (0, 4, False)] for k in KEYS}
+VSH = {"S": 0.5, "D": 0.3}
+SIGN_AT = {1: 0, 2: 1}
+SORT_AT = {1: 0, 2: 1}
+Y0 = "av"
+HEAD = "v:0:48 a:48:96 v:96:136 a:136:192 p:0:96 p:96:136 p:136:192 c0 g0 g1 sv0 sa1 c1 x0 m0 g2 x1 m1 g3 "
+TAIL = HEAD + "sa2 x2 m2 sa3 x3 m3 kv0 ka1 kv2 ka3"
+TAIL_LAST = HEAD + "ka0 ka1 sv2 x2 m2 sa3 x3 m3 kv2 ka3"
+
+
+def split(engs, n):
+    parts = [list(engs)]
+    while len(parts) < n:
+        big = max(len(p) for p in parts)
+        i = max(j for j, p in enumerate(parts) if len(p) == big)
+        p = parts[i]
+        parts[i:i + 1] = [p[:big // 2], p[big // 2:]]
+    return parts
+
+
+def bits(engs):
+    m = 0
+    for e in engs:
+        m |= 1 << e
+    return m
+
+
+def ones(m):
+    return bin(m).count("1")
+
+
+def plan(T, topo, rank):
+    n = len(T.cores)
+    me = T.cores[rank]
+    dests = [(d, T.cores[(rank + 1 + d) % n]) for d in range(n - 1)]
+    dests.sort(key=lambda x: not topo.same_plane(me, x[1]))
+    handed = set()
+    for calls in CALLS.values():
+        pos = 0
+        for nr, nd, wide in calls:
+            handed.update(range(pos, pos + nr))
+            pos += nr + nd
+    free = sorted((c for c in topo.cores_of(me) if T.rank_of(c) is None), key=lambda c: topo.die(c) == topo.die(me))
+    helper = {}
+    for i in sorted(handed, reverse=True):
+        helper[i] = [h for h in free if topo.may_write(h, dests[i][1])][0]
+        free.remove(helper[i])
+    off = topo.engines(me, dests[0][1])
+    out = {}
+    for k, calls in CALLS.items():
+        pos, out[k] = 0, []
+        for nr, nd, wide in calls:
+            c = []
+            if nr:
+                on = topo.engines(me, helper[pos])
+                parts = split(on if wide else [e for e in on if e not in off], nr)
+                c += [(pos + i,) + dests[pos + i] + (helper[pos + i], bits(parts[i])) for i in range(nr)]
+            if nd:
+                parts = split(off, nd)
+                c += [(pos + nr + i,) + dests[pos + nr + i] + (None, bits(parts[i])) for i in range(nd)]
+            out[k].append(c)
+            pos += nr + nd
+    return [d for d, c in dests], out
+
+
+def helper_program(g, core, T, topo):
+    for r, c in enumerate(T.cores):
+        if core not in topo.cores_of(c):
+            continue
+        calls, total = plan(T, topo, r)[1], 0
+        for k in KEYS:
+            for pos, d, dest, h, m in [x for call in calls[k] for x in call if x[3] == core]:
+                rid, pid = topo.addr(dest, core)
+                win, ar = T[k], T.sem["ar" + k]
+                g.wait_ge(ar, ones(m))
+                g.remote_dma(win[:, A + SG * d:A + SG * (d + 1)], win[:, 0:SG], ar, T.sem.sentS, pid, rid, topo.mask(core, dest))
+                total += ones(topo.mask(core, dest))
+        if total:
+            g.wait_ge(T.sem.sentS, total)
+
+
+def rank_program(g, core, T, topo):
+    rank = T.rank_of(core)
+    if rank is None:
+        helper_program(g, core, T, topo)
+        return
+    OP, AF = AluOpType, ActivationFunctionType
+    order, calls = plan(T, topo, rank)
+    arrive = {k: 0 for k in KEYS}
+    for r in range(len(T.cores)):
+        if r != rank:
+            for k, cs in plan(T, topo, r)[1].items():
+                arrive[k] += sum(ones(m if h is None else topo.mask(h, core))
+                                 for call in cs for pos, d, dest, h, m in call if dest == core)
+
+    Q = {"g": g, "pe": g.tensor, "v": g.vector, "a": g.scalar, "s": g.sync}
+    cnt = {}
+    seen = {q: {} for q in Q}
+    clock = {}
+    acc = {}
+
+    def wait(q, tok):
+        if seen[q].get(tok[0], 0) >= tok[1]:
+            return
+        Q[q].wait_ge(T.sem[tok[0]], tok[1])
+        for s, v in clock.get(tok, {tok[0]: tok[1]}).items():
+            if seen[q].get(s, 0) < v:
+                seen[q][s] = v
+
+    def note(tok, rd, wr):
+        for n, lo, hi in wr:
+            acc[n] = [e for e in acc.get(n, []) if not (lo <= e[0] and e[1] <= hi)] + [(lo, hi, True, tok)]
+        for n, lo, hi in rd:
+            acc.setdefault(n, []).append((lo, hi, False, tok))
+
+    def op(q, fn, rd, wr, sem=None, inc=1, mark=True):
+        wr = wr + [(n, 0, 512) for n, lo, hi in rd if n[0:2] in ("pv", "ps", "pd")]
+        need = {}
+        for lst, isw in ((rd, False), (wr, True)):
+            for n, lo, hi in lst:
+                for e in acc.get(n, []):
+                    if e[0] < hi and lo < e[1] and (isw or e[2]):
+                        if q == "pe" and e[3][0] == "c_pe" and isw:
+                            continue
+                        need[e[3][0]] = max(need.get(e[3][0], 0), e[3][1])
+        for s in sorted(need, key=lambda s: s == "c_" + q):
+            wait(q, (s, need[s]))
+        ins = fn()
+        if not mark:
+            return
+        s = sem or "c_" + q
+        cnt[s] = cnt.get(s, 0) + inc
+        if ins is not None:
+            ins.then_inc(T.sem[s], inc)
+        tok = (s, cnt[s])
+        clock[tok] = dict(seen[q])
+        clock[tok][s] = cnt[s]
+        note(tok, rd, wr)
+
+    def rg(*a):
+        return [tuple(a[i:i + 3]) for i in range(0, len(a), 3)]
+
+    V, S = g.vector, g.scalar
+
+    def dma(q, out, in_, rd, wr, sem):
+        op(q, lambda: Q[q].dma_start(out, in_), rd, wr, sem=sem, inc=16)
+
+    def mm(bank, lo, hi, terms, first=True, last=True):
+        rd = [x for t3 in terms for x in t3[2]]
+
+        def fn():
+            ins = None
+            for i, (l, r, _) in enumerate(terms):
+                ins = g.tensor.matmul(T[bank][:, lo:hi], l, r, first and i == 0, last and i == len(terms) - 1)
+            return ins
+        op("pe", fn, rd, rg(bank, 0, 512))
+
+    def ts(out, in0, s1, s2, o0, o1, rd, wr):
+        if s2 is None:
+            op("v", lambda: V.tensor_scalar(out, in0, s1, None, o0), rd, wr)
+        else:
+            op("v", lambda: V.tensor_scalar(out, in0, s1, s2, o0, o1), rd, wr)
+
+    def tt(out, in0, in1, o, rd, wr):
+        op("v", lambda: V.tensor_tensor(out, in0, in1, o), rd, wr)
+
+    def scan(out, d0, d1, o0, rd, wr):
+        op("v", lambda: V.tensor_tensor_scan(out, d0, d1, 0.0, o0, OP.max), rd, wr)
+
+    def cp(q, out, in_, rd, wr, add=None):
+        if q == "v":
+            if add is None:
+                op("v", lambda: V.tensor_copy(out, in_), rd, wr)
+            else:
+                ts(out, in_, add, None, OP.add, None, rd, wr)
+        elif add is None:
+            op("a", lambda: S.activation(out, in_, AF.Copy), rd, wr)
+        else:
+            op("a", lambda: S.activation(out, in_, AF.Identity, bias=add), rd, wr)
+
+    def gather(q, dst, d0, win, wn, off, c0, c1, times=None):
+        if c1 <= c0:
+            return
+        n = 16 * (c1 - c0)
+        src = T[win][:, 0:wn].indirect(T[off][:, c0:c1])
+        rd, wr = rg(win, 0, wn, off, c0, c1), rg(dst, d0, d0 + n)
+        if times is None:
+            cp(q, T[dst][:, d0:d0 + n], src, rd, wr)
+        else:
+            tt(T[dst][:, d0:d0 + n], src, T[times][:, d0:d0 + n], OP.mult, rd + rg(times, d0, d0 + n), wr)
+
+    def iota(n, w, pattern, base, cm):
+        op("g", lambda: g.iota(T[n][:, 0:w], pattern, base, cm, allow_small_or_imprecise_dtypes=True), [], rg(n, 0, w))
+
+    def term(m, n, lo, hi, step=1):
+        return (T[m][:], T[n][:, lo:hi:step], rg(m, 0, 128, n, lo, hi))
+
+    for k in KEYS:
+        note(("ar" + k, arrive[k]), [], rg(k, A, W))
+
+    dma("s", T.hap[:, 0:1024], T.haps[:, 0:1024], [], rg("hap", 0, 1024), "l_h0")
+    dma("s", T.hap[:, 1024:2048], T.haps[:, 1024:2048], [], rg("hap", 1024, 2048), "l_h1")
+    dma("s", T.gl[:], T.gift[:], [], rg("gl", 0, 210), "l_gl")
+    dma("s", T.dl[:], T.dam[:], [], rg("dl", 0, 192), "l_dl")
+    dma("s", T.rl[:, 0:192], T.rival[:, 0:192], [], rg("rl", 0, 192), "l_r0")
+    dma("s", T.ef[:, 0:1], T.eff[:], [], rg("ef", 0, 1), "l_ef")
+    dma("s", T.rl[:, 192:576], T.rival[:, 192:576], [], rg("rl", 192, 576), "l_r1")
+    iota("iot", 128, [[1, 128]], 0, -1)
+    op("g", lambda: g.iota(T.pc[:, 0:1], [[1, 1]], 0, 1), [], rg("pc", 0, 1))
+    iota("zz", 96, [[0, 3], [2, 32]], -17, -2)
+    iota("kk", 96, [[0, 32], [-1, 3]], 2, 0)
+    iota("jb", 8, [[32, 8]], 0, 0)
+    iota("cid", 192, [[217, 3], [1200, 64]], 0, 75)
+    iota("cir", 576, [[217, 3], [1200, 64], [0, 3]], 389, 75)
+    ts(T.idn[:], T.iot[:], 0.0, None, OP.is_equal, None, rg("iot", 0, 128), rg("idn", 0, 128))
+    ts(T.nid[:], T.iot[:], 0.0, -1.0, OP.is_equal, OP.mult, rg("iot", 0, 128), rg("nid", 0, 128))
+    ts(T.hid[:], T.iot[:], 0.0, 0.5, OP.is_equal, OP.mult, rg("iot", 0, 128), rg("hid", 0, 128))
+    op("v", lambda: V.memset(T.bm[:], 0.0), [], rg("bm", 0, 144))
+    ts(T.pc[:, 1:2], T.pc[:, 0:1], 112, None, OP.bitwise_and, None, rg("pc", 0, 1), rg("pc", 1, 2))
+    ts(T.cols[:, 0:1], T.pc[:, 1:2], 2.0, None, OP.mult, None, rg("pc", 1, 2), rg("cols", 0, 1))
+    ts(T.cols[:, 1:2], T.pc[:, 1:2], -75.0, None, OP.mult, None, rg("pc", 1, 2), rg("cols", 1, 2))
+    ts(T.rst[:], T.kk[:], 2.0, -4194304.0, OP.is_equal, OP.mult, rg("kk", 0, 96), rg("rst", 0, 96))
+    ts(T.tie[:], T.kk[:], 0.25, None, OP.mult, None, rg("kk", 0, 96), rg("tie", 0, 96))
+    op("a", lambda: S.activation(T.za[:], T.zz[:], AF.Abs, bias=T.cols[:, 0:1]), rg("zz", 0, 96, "cols", 0, 1), rg("za", 0, 96))
+    op("a", lambda: S.activation(T.tab[:], T.za[:], AF.Sign, bias=16.0, scale=-1.0), rg("za", 0, 96), rg("tab", 0, 96))
+
+    def gift_lists(t):
+        pos, cutat = 0, [i for i in range(1, len(order)) if order[i] < order[i - 1]]
+        for ds in [order[i:j] for i, j in zip([0] + cutat, cutat + [len(order)])]:
+            step = ds[1] - ds[0] if len(ds) > 1 else 1
+            runs = [ds] if all(ds[i] == ds[0] + i * step for i in range(len(ds))) else [[d] for d in ds]
+            for run in runs:
+                lo, hi = 70 * t + 10 * pos, 70 * t + 10 * (pos + len(run))
+                cp("v", T.goff[:, lo:hi], T.gl[:, 7 * t + run[0]:7 * t + run[-1] + 1:step, :], rg("gl", 0, 210), rg("goff", lo, hi))
+                pos += len(run)
+
+    def gifts(k, t):
+        win, buf, sent = "%s%d" % (k, t), "g" + k, "sent" + k
+        o, total, ar = 70 * t, 0, T.sem["ar" + win]
+        for ci, call in enumerate(calls[win]):
+            lo, hi = 10 * call[0][0], 10 * (call[-1][0] + 1)
+            mid = lo + 2 * int(round((hi - lo) * VSH[k] / 2))
+            gather("v", buf, 16 * lo, win, A, "goff", o + lo, o + mid)
+            gather("a", buf, 16 * mid, win, A, "goff", o + mid, o + hi)
+            tr = []
+            for pos, d, dest, h, m in call:
+                rid, pid = topo.addr(dest if h is None else h, core)
+                at = A + SG * d if h is None else 0
+                tr.append(RemoteDMATransfer(dst_ids=[DstId(rid=rid, pnc=pid)], dma_engine_mask=m, remote_sem=ar,
+                                            src=T[buf][:, SG * pos:SG * (pos + 1)], dst=T[win][:, at:at + SG]))
+                total += ones(m)
+
+            def fn():
+                g.remote_dma_fused(tr, local_sem=T.sem[sent])
+            if ci + 1 < len(calls[win]):
+                op("g", fn, rg(buf, 16 * lo, 16 * hi), [], mark=False)
+            else:
+                op("g", fn, rg(buf, 0, 1120), [], sem=sent, inc=total)
+
+    def cross(src, o, ci, co):
+        ts(T.ta[:], T[src][:, o:o + 192], 181.0, T.cols[:, 1:2], OP.mult, OP.add, rg(src, o, o + 192, "cols", 1, 2), rg("ta", 0, 192))
+        yield
+        tt(T.ti[:], T.ta[:], T[ci][:, co:co + 192], OP.add, rg("ta", 0, 192, ci, co, co + 192), rg("ti", 0, 192))
+        yield
+        ts(T.tj[:], T.ti[:], 5, 31, OP.logical_shift_right, OP.bitwise_and, rg("ti", 0, 192), rg("tj", 0, 192))
+        yield
+
+    def dam_lists():
+        cp("v", T.doff[:], T.dl[:], rg("dl", 0, 192), rg("doff", 0, 192))
+        yield
+        yield from cross("dl", 0, "cid", 0)
+        cp("v", T.dz[:], T.tj[:], rg("tj", 0, 192), rg("dz", 0, 192))
+        yield
+
+    def sort_rivals(t):
+        o = 192 * t
+        a, b, c = (T.rl[:, o + 64 * k:o + 64 * (k + 1)] for k in range(3))
+        rr = rg("rl", o, o + 192)
+        tt(T.tb[:, 0:64], a, b, OP.max, rr, rg("tb", 0, 64))
+        yield
+        tt(T.tb[:, 64:128], a, b, OP.min, rr, rg("tb", 64, 128))
+        yield
+        tt(T.tb[:, 128:192], T.tb[:, 0:64], c, OP.min, rr + rg("tb", 0, 64), rg("tb", 128, 192))
+        yield
+        tt(T.rs[:, o:o + 192:3], T.tb[:, 0:64], c, OP.max, rr + rg("tb", 0, 64), rg("rs", o, o + 1))
+        tt(T.rs[:, o + 2:o + 192:3], T.tb[:, 64:128], c, OP.min, rr + rg("tb", 64, 128), rg("rs", o + 2, o + 3))
+        tt(T.rs[:, o + 1:o + 192:3], T.tb[:, 64:128], T.tb[:, 128:192], OP.max, rg("tb", 64, 192),
+           rg("rs", o + 1, o + 2, "rs", o + 3, o + 192))
+        yield
+        cp("v", T.roff[:, o:o + 192], T.rs[:, o:o + 192], rg("rs", o, o + 192), rg("roff", o, o + 192))
+        yield
+
+    def rival_cross(t):
+        yield from cross("rs", 192 * t, "cir", 192 * t)
+        for k in range(3):
+            ts(T.u2[:, k:192:3], T.tj[:, k:192:3], 32.0 * (2 - k), None, OP.add, None, rg("tj", 0, 192),
+               rg("u2", k, k + 1) if k != 1 else rg("u2", 1, 2, "u2", 3, 192))
+        yield
+
+    def weave(*gens):
+        gens = list(gens)
+        while gens:
+            gens = [x for x in gens if next(x, 1) is None]
+
+    def dam_signs(t):
+        gather("a", "sgd%d" % t, 0, "tab", 96, "dz", 64 * t, 64 * (t + 1))
+
+    def values(bank, base, c0, c1):
+        terms = [(T.idn[:], T.tie[:, c0 - base:c1 - base], rg("idn", 0, 128, "tie", 0, 96))]
+        for q in range(16):
+            terms.append((T.bm[:, 15 - q:143 - q], T.R[:, 16 * c0 + q:16 * c1:16], rg("bm", 0, 144, "R", 16 * c0, 16 * c1)))
+        mm(bank, c0 - base, c1 - base, terms)
+
+    def choose(t, h):
+        bank, o, s0 = "pv%d" % h, 192 * t + 96 * h, 64 * h
+        pv = T[bank][:, 0:96]
+        scan(T.M[:], T.rst[:], pv, OP.add, rg("rst", 0, 96, bank, 0, 96), rg("M", 0, 96))
+        tt(T.nf[:], pv, T.M[:], OP.not_equal, rg(bank, 0, 96, "M", 0, 96), rg("nf", 0, 96))
+        scan(T.sel[:, 96:192], T.nf[:], T.u2[:, 96 * h:96 * (h + 1)], OP.mult, rg("nf", 0, 96, "u2", 0, 192), rg("sel", 96, 192))
+        scan(T.sel[:, 0:96], T.nf[:], T.rs[:, o:o + 96], OP.mult, rg("nf", 0, 96, "rs", 192 * t, 192 * t + 192), rg("sel", 0, 96))
+        cp("v", T.so[:, s0:s0 + 64], T.sel[:, 2:192:3], rg("sel", 0, 192), rg("so", s0, s0 + 64))
+
+    for q in range(4):
+        mm("ps%d" % q, 0, 256, [term("idn", "hap", 512 * q, 512 * (q + 1), 2), term("idn", "hap", 512 * q + 1, 512 * (q + 1), 2)])
+    for h in range(2):
+        mm("pd%d" % h, 0, 512, [term("idn", "hap", 1024 * h, 1024 * (h + 1), 2), term("nid", "hap", 1024 * h + 1, 1024 * (h + 1), 2)])
+    for q, e in ((0, "a"), (1, "v"), (2, "a"), (3, "v")):
+        cp(e, T.S0[:, 256 * q:256 * (q + 1)], T["ps%d" % q][:, 0:256], rg("ps%d" % q, 0, 256), rg("S0", 256 * q, 256 * (q + 1)), add=-255.0)
+    gift_lists(0)
+
+    for t in range(G):
+        Sw, Dw, last = "S%d" % t, "D%d" % t, t == G - 1
+        gifts("S", t)
+        for h, e in ((0, "a"), (1, "v")):
+            cp(e, T[Dw][:, 512 * h:512 * (h + 1)], T["pd%d" % h][:], rg("pd%d" % h, 0, 512), rg(Dw, 512 * h, 512 * (h + 1)))
+        gifts("D", t)
+        if t == 0:
+            cp("v", T.cols[:, 2:3], T.ef[:, 0:1], rg("ef", 0, 1), rg("cols", 2, 3))
+            weave(dam_lists(), sort_rivals(0))
+            ts(T.bm[:, 15:143:16], T.jb[:], T.cols[:, 0:1], T.cols[:, 2:3], OP.is_equal, OP.mult,
+               rg("jb", 0, 8, "cols", 0, 3), rg("bm", 0, 144))
+        gather("a", "Sd", 0, Sw, A, "doff", 64 * t, 64 * (t + 1))
+        if t == 0:
+            dam_signs(0)
+        else:
+            gather("v", "Xd", 0, Dw, A, "doff", 64 * t, 64 * (t + 1), times="sgd%d" % t)
+        weave(rival_cross(t), *[sort_rivals(u) for u in range(t + 1, G) if SORT_AT[u] == t])
+        if t == 0:
+            gather("v", "Xd", 0, Dw, A, "doff", 0, 64, times="sgd0")
+        if not last:
+            gift_lists(t + 1)
+            for u in range(t + 1, G):
+                if SIGN_AT[u] == t:
+                    dam_signs(u)
+            for q in range(4):
+                mm("ps%d" % q, 0, 256, [term("hid", "Sd", 256 * q, 256 * (q + 1)), term("hid", "Xd", 256 * q, 256 * (q + 1))], last=False)
+            for h in range(2):
+                mm("pd%d" % h, 0, 512, [term("idn", "Sd", 512 * h, 512 * (h + 1)), term("idn", "Xd", 512 * h, 512 * (h + 1))], last=False)
+        else:
+            for h in range(2):
+                mm("pd%d" % h, 0, 512, [term("hid", "Sd", 512 * h, 512 * (h + 1)), term("hid", "Xd", 512 * h, 512 * (h + 1))])
+                cp(Y0[h], T.hap[:, 1024 * h:1024 * (h + 1):2], T["pd%d" % h][:], rg("pd%d" % h, 0, 512),
+                   rg("hap", 1024 * h, 1024 * (h + 1)), add=127.5)
+        o = 192 * t
+        for w in (TAIL_LAST if last else TAIL).split():
+            if ":" in w:
+                e, c0, c1 = w.split(":")
+                c0, c1 = int(c0), int(c1)
+                if e == "p":
+                    values("pv%d" % (c0 // 96), 96 * (c0 // 96), c0, c1)
+                else:
+                    gather(e, "R", 16 * c0, Sw, W, "roff", o + c0, o + c1)
+                continue
+            q = int(w[-1])
+            c, lo, hi, b = 64 * (q // 2) + 16 * (q % 2), 256 * q, 256 * (q + 1), "ps%d" % q
+            if w[0] == "c":
+                choose(t, q)
+            elif w[0] == "g":
+                gather("a", "sgs", lo, "tab", 96, "so", c + 32, c + 48)
+            elif w[0] == "s":
+                gather(w[1], "Ss", lo, Sw, W, "so", c, c + 16)
+            elif w[0] == "x":
+                gather("v", "Xs", lo, Dw, W, "so", c, c + 16, times="sgs")
+            elif w[0] == "m":
+                mm(b, 0, 256, [term("hid", "Ss", lo, hi), term("hid", "Xs", lo, hi)], first=last)
+            elif last:
+                cp(w[1], T.hap[:, 2 * lo + 1:2 * hi:2], T[b][:, 0:256], rg(b, 0, 256), rg("hap", 2 * lo, 2 * hi), add=127.5)
+                dma("s", T.y[:, 2 * lo:2 * hi], T.hap[:, 2 * lo:2 * hi], rg("hap", 2 * lo, 2 * hi), [], "st")
+            else:
+                n = "S%d" % (t + 1)
+                cp(w[1], T[n][:, lo:hi], T[b][:, 0:256], rg(b, 0, 256), rg(n, lo, hi))
+        if not last:
+            n = "S%d" % (t + 1)
+            for h in range(2):
+                mm("pd%d" % h, 0, 512, [term("nid", n, 512 * h, 512 * (h + 1))], first=False)
+
+    for s in sorted(cnt, key=lambda s: s == "st"):
+        wait("g", (s, cnt[s]))

@@ -4,29 +4,36 @@ from concourse.mybir import AluOpType, ActivationFunctionType
 A, SG, G, W = 1024, 160, 3, 2144
 BF, F32, I32, U16 = "bfloat16", "float32", "int32", "uint16"
 SCRATCH = {}
-for _d, _l in ((BF, "hap:2048 iot:128 idn:128 nid:128 hid:128 ef:16 bm:144 tab:96 tie:96 gS:1120 gD:1120 R:3072 "
+for _d, _l in ((BF, "hap:2048 iot:128 idn:128 nid:128 hid:128 two:128 mid:512 ef:16 bm:144 tab:96 gS:1120 gD:1120 R:3072 "
                     "sgd0:1024 sgd1:1024 sgd2:1024 Sd:1024 Xd:1024 sgs:1024 Ss:1024 Xs:1024 "
                     "S0:2144 S1:2144 S2:2144 D0:2144 D1:2144 D2:2144"),
-               (F32, "rs:576 u2:192 ta:192 tb:192 cid:192 cir:576 cols:8 jb:8 zz:96 za:96 kk:96 rst:96 M:96 nf:96 sel:192"),
-               (I32, "dl:192 rl:576 ti:192 tj:192 pc:8"),
-               (U16, "goff:210 doff:192 dz:192 roff:576 so:128")):
+               (F32, "rs:576 u2:576 tb:192 cid:192 cir:576 cols:8 jb:8 zz:96 za:96 kk:144 rst:144 M:192 nf:192 sel:384"),
+               (I32, "dl:192 ti:576 tj:576 di:192 dj:192 pc:8"),
+               (U16, "goff:210 gev:70 god:70 doff:192 dz:192 roff:576 so:128")):
     for _x in _l.split():
         SCRATCH[_x.split(":")[0]] = ("sbuf", [128, int(_x.split(":")[1])], _d)
-SCRATCH["gl"] = ("sbuf", [128, 21, 10], I32)
+SCRATCH["gl"] = ("sbuf", [128, G, 7, 10], I32)
+SCRATCH["rl"] = ("sbuf", [128, G, 3, 64], I32)
 for _n in ("pv0", "pv1", "ps0", "ps1", "ps2", "ps3", "pd0", "pd1"):
     SCRATCH[_n] = ("psum", [128, 512], F32)
 KEYS = ["%s%d" % (k, t) for t in range(G) for k in "SD"]
-SEMAPHORES = (["c_pe", "c_v", "c_a", "c_g", "l_h0", "l_h1", "l_gl", "l_dl", "l_ef", "l_r0", "l_r1", "st", "sentS", "sentD"]
+SEMAPHORES = (["c_pe", "c_v", "c_a", "c_g", "l_h0", "l_h1", "l_gl", "l_dl", "l_ef", "l_rl", "st", "sentS", "sentD"]
               + ["ar" + k for k in KEYS])
 
 CALLS = {k: [(3, 0, k[0] == "S"), (0, 4, False)] for k in KEYS}
-VSH = {"S": 0.5, "D": 0.3}
-SIGN_AT = {1: 0, 2: 1}
-SORT_AT = {1: 0, 2: 1}
-Y0 = "av"
-HEAD = "v:0:48 a:48:96 v:96:136 a:136:192 p:0:96 p:96:136 p:136:192 c0 g0 g1 sv0 sa1 c1 x0 m0 g2 x1 m1 g3 "
-TAIL = HEAD + "sa2 x2 m2 sa3 x3 m3 kv0 ka1 kv2 ka3"
-TAIL_LAST = HEAD + "ka0 ka1 sv2 x2 m2 sa3 x3 m3 kv2 ka3"
+CALLS["S0"] = [(0, 1, False), (0, 2, False), (0, 4, False)]
+VSH = {"S0": 0.6, "D0": 0.4, "S1": 0.5, "D1": 0.5, "S2": 0.5, "D2": 0.3}
+LOADS = "s:h0 a:gl a:h1 s:dl s:rl s:ef"
+HALF = [30, 30, 30]
+PIECES = [[0, 8, 30, 56, 64], [0, 8, 30, 56, 64], [0, 16, 30, 50, 64]]
+DAMS = " Sa:0:32 X:0:32 M0 M1 Sa:32:64 X:32:64 M2 M3 "
+HERE = (" rv:0:44 ra:44:90 p:0:90 rv:90:136 ra:136:192 za%d:44:64 A0 B0 C0 D0 p:90:192 N0 N1 A1 B1 C1 D1 ga:0:30 sa:0:30 x:0:30"
+        " ga:42:64 gv:30:42 sa:30:58 m0 m1 x:42:64 x:30:42 sa:58:64 m2 K0 ka1 m3 ka3 K2 n0 n1")
+STEPS = ["L:gift ev0 GS0 ea1 GS1 GS2 L:dam da0 da1 E GD0 za0:0:64 L:sort" + DAMS + "L:x0 GD1 za1:0:44" + HERE % 1,
+         "GS0 GS1 da0 dv1 GD0" + DAMS + "GD1 L:x1 za2:0:44" + HERE % 2,
+         "GS0 GS1 da0 dv1 GD0 Sa:0:32 X:0:32 N0 Sa:32:64 X:32:64 N1 GD1 L:x2 ya1"
+         " rv:0:46 ra:46:90 rv:90:136 ra:136:192 p:0:90 ya0 A0 B0 C0 D0 ga:0:30 p:90:192 A1 B1 sa:0:30 C1 D1 ga:30:50 x:0:30"
+         " m0 sa:30:50 m1 m2 K0 x:30:50 ka1 gv:50:64 sa:50:64 K2 x:50:64 m3 K3"]
 
 
 def split(engs, n):
@@ -128,21 +135,25 @@ def rank_program(g, core, T, topo):
             if seen[q].get(s, 0) < v:
                 seen[q][s] = v
 
+    def bank(n):
+        return SCRATCH[n][0] == "psum"
+
     def note(tok, rd, wr):
+        for n, lo, hi in rd + wr:
+            if bank(n):
+                acc[n] = [e for e in acc.get(n, []) if e[3][0] == tok[0]]
         for n, lo, hi in wr:
             acc[n] = [e for e in acc.get(n, []) if not (lo <= e[0] and e[1] <= hi)] + [(lo, hi, True, tok)]
         for n, lo, hi in rd:
             acc.setdefault(n, []).append((lo, hi, False, tok))
 
     def op(q, fn, rd, wr, sem=None, inc=1, mark=True):
-        wr = wr + [(n, 0, 512) for n, lo, hi in rd if n[0:2] in ("pv", "ps", "pd")]
         need = {}
         for lst, isw in ((rd, False), (wr, True)):
             for n, lo, hi in lst:
                 for e in acc.get(n, []):
-                    if e[0] < hi and lo < e[1] and (isw or e[2]):
-                        if q == "pe" and e[3][0] == "c_pe" and isw:
-                            continue
+                    other = bank(n) and e[3][0] != "c_" + q
+                    if other or (e[0] < hi and lo < e[1] and (isw or e[2]) and not (q == "pe" and e[3][0] == "c_pe")):
                         need[e[3][0]] = max(need.get(e[3][0], 0), e[3][1])
         for s in sorted(need, key=lambda s: s == "c_" + q):
             wait(q, (s, need[s]))
@@ -166,15 +177,15 @@ def rank_program(g, core, T, topo):
     def dma(q, out, in_, rd, wr, sem):
         op(q, lambda: Q[q].dma_start(out, in_), rd, wr, sem=sem, inc=16)
 
-    def mm(bank, lo, hi, terms, first=True, last=True):
+    def mm(b, lo, hi, terms, first=True, last=True):
         rd = [x for t3 in terms for x in t3[2]]
 
         def fn():
             ins = None
             for i, (l, r, _) in enumerate(terms):
-                ins = g.tensor.matmul(T[bank][:, lo:hi], l, r, first and i == 0, last and i == len(terms) - 1)
+                ins = g.tensor.matmul(T[b][:, lo:hi], l, r, first and i == 0, last and i == len(terms) - 1)
             return ins
-        op("pe", fn, rd, rg(bank, 0, 512))
+        op("pe", fn, rd, rg(b, lo, hi))
 
     def ts(out, in0, s1, s2, o0, o1, rd, wr):
         if s2 is None:
@@ -219,103 +230,130 @@ def rank_program(g, core, T, topo):
     for k in KEYS:
         note(("ar" + k, arrive[k]), [], rg(k, A, W))
 
-    dma("s", T.hap[:, 0:1024], T.haps[:, 0:1024], [], rg("hap", 0, 1024), "l_h0")
-    dma("s", T.hap[:, 1024:2048], T.haps[:, 1024:2048], [], rg("hap", 1024, 2048), "l_h1")
-    dma("s", T.gl[:], T.gift[:], [], rg("gl", 0, 210), "l_gl")
-    dma("s", T.dl[:], T.dam[:], [], rg("dl", 0, 192), "l_dl")
-    dma("s", T.rl[:, 0:192], T.rival[:, 0:192], [], rg("rl", 0, 192), "l_r0")
-    dma("s", T.ef[:, 0:1], T.eff[:], [], rg("ef", 0, 1), "l_ef")
-    dma("s", T.rl[:, 192:576], T.rival[:, 192:576], [], rg("rl", 192, 576), "l_r1")
+    loads = {"h0": (T.hap[:, 0:1024], T.haps[:, 0:1024], rg("hap", 0, 1024)), "h1": (T.hap[:, 1024:2048], T.haps[:, 1024:2048], rg("hap", 1024, 2048)),
+             "gl": (T.gl[:], T.gift[:], rg("gl", 0, 210)), "rl": (T.rl[:], T.rival[:], rg("rl", 0, 576)),
+             "dl": (T.dl[:], T.dam[:], rg("dl", 0, 192)), "ef": (T.ef[:, 0:1], T.eff[:], rg("ef", 0, 1))}
+    for w in LOADS.split():
+        q, n = w.split(":")
+        dma(q, loads[n][0], loads[n][1], [], loads[n][2], "l_" + n)
     iota("iot", 128, [[1, 128]], 0, -1)
     op("g", lambda: g.iota(T.pc[:, 0:1], [[1, 1]], 0, 1), [], rg("pc", 0, 1))
     iota("zz", 96, [[0, 3], [2, 32]], -17, -2)
-    iota("kk", 96, [[0, 32], [-1, 3]], 2, 0)
+    iota("kk", 144, [[0, 48], [-1, 3]], 2, 0)
     iota("jb", 8, [[32, 8]], 0, 0)
     iota("cid", 192, [[217, 3], [1200, 64]], 0, 75)
     iota("cir", 576, [[217, 3], [1200, 64], [0, 3]], 389, 75)
     ts(T.idn[:], T.iot[:], 0.0, None, OP.is_equal, None, rg("iot", 0, 128), rg("idn", 0, 128))
     ts(T.nid[:], T.iot[:], 0.0, -1.0, OP.is_equal, OP.mult, rg("iot", 0, 128), rg("nid", 0, 128))
     ts(T.hid[:], T.iot[:], 0.0, 0.5, OP.is_equal, OP.mult, rg("iot", 0, 128), rg("hid", 0, 128))
+    ts(T.two[:], T.iot[:], 0.0, 2.0, OP.is_equal, OP.mult, rg("iot", 0, 128), rg("two", 0, 128))
     op("v", lambda: V.memset(T.bm[:], 0.0), [], rg("bm", 0, 144))
+    op("v", lambda: V.memset(T.mid[:], 127.5), [], rg("mid", 0, 512))
     ts(T.pc[:, 1:2], T.pc[:, 0:1], 112, None, OP.bitwise_and, None, rg("pc", 0, 1), rg("pc", 1, 2))
     ts(T.cols[:, 0:1], T.pc[:, 1:2], 2.0, None, OP.mult, None, rg("pc", 1, 2), rg("cols", 0, 1))
     ts(T.cols[:, 1:2], T.pc[:, 1:2], -75.0, None, OP.mult, None, rg("pc", 1, 2), rg("cols", 1, 2))
-    ts(T.rst[:], T.kk[:], 2.0, -4194304.0, OP.is_equal, OP.mult, rg("kk", 0, 96), rg("rst", 0, 96))
-    ts(T.tie[:], T.kk[:], 0.25, None, OP.mult, None, rg("kk", 0, 96), rg("tie", 0, 96))
+    ts(T.rst[:], T.kk[:], 2.0, -4194304.0, OP.is_equal, OP.mult, rg("kk", 0, 144), rg("rst", 0, 144))
+    ts(T.rst[:], T.rst[:], 0.25, None, OP.add, None, rg("rst", 0, 144), rg("rst", 0, 144))
     op("a", lambda: S.activation(T.za[:], T.zz[:], AF.Abs, bias=T.cols[:, 0:1]), rg("zz", 0, 96, "cols", 0, 1), rg("za", 0, 96))
-    op("a", lambda: S.activation(T.tab[:], T.za[:], AF.Sign, bias=16.0, scale=-1.0), rg("za", 0, 96), rg("tab", 0, 96))
+    ts(T.tab[:], T.za[:], 16.0, 0.5, OP.is_lt, OP.subtract, rg("za", 0, 96), rg("tab", 0, 96))
 
-    def gift_lists(t):
-        pos, cutat = 0, [i for i in range(1, len(order)) if order[i] < order[i - 1]]
-        for ds in [order[i:j] for i, j in zip([0] + cutat, cutat + [len(order)])]:
-            step = ds[1] - ds[0] if len(ds) > 1 else 1
-            runs = [ds] if all(ds[i] == ds[0] + i * step for i in range(len(ds))) else [[d] for d in ds]
-            for run in runs:
-                lo, hi = 70 * t + 10 * pos, 70 * t + 10 * (pos + len(run))
-                cp("v", T.goff[:, lo:hi], T.gl[:, 7 * t + run[0]:7 * t + run[-1] + 1:step, :], rg("gl", 0, 210), rg("goff", lo, hi))
-                pos += len(run)
+    runs = []
+    for d in order:
+        if runs and d > runs[-1][-1] and (len(runs[-1]) == 1 or d - runs[-1][-1] == runs[-1][1] - runs[-1][0]):
+            runs[-1].append(d)
+        else:
+            runs.append([d])
+    starts = [sum(len(r) for r in runs[:i]) for i in range(len(runs) + 1)]
 
-    def gifts(k, t):
+    def gift_lists():
+        for run, pos in zip(runs, starts):
+            lo, hi, step = 10 * G * pos, 10 * G * (pos + len(run)), run[1] - run[0] if len(run) > 1 else 1
+            cp("v", T.goff[:, lo:hi], T.gl[:, :, run[0]:run[-1] + 1:step, :], rg("gl", 0, 210), rg("goff", lo, hi))
+            yield
+
+    def first_lists():
+        for pos, d, dest, h, m in calls["S0"][0]:
+            lo, hi = 10 * pos, 10 * (pos + 1)
+            for n, s in (("gev", 0.0), ("god", 1.0)):
+                ts(T[n][:, lo:hi], T.gl[:, 0, d, :], 2.0, s, OP.mult, OP.add, rg("gl", 0, 210), rg(n, lo, hi))
+
+    def first_sums(lo, hi):
+        for a in range(lo, hi, 20):
+            b = min(a + 20, hi)
+            op("a", lambda: S.activation(T.R[:, 16 * a:16 * b], T.hap[:].indirect(T.gev[:, a:b]), AF.Identity, bias=-255.0),
+               rg("hap", 0, 2048, "gev", a, b), rg("R", 16 * a, 16 * b))
+            tt(T.gS[:, 16 * a:16 * b], T.hap[:].indirect(T.god[:, a:b]), T.R[:, 16 * a:16 * b], OP.add,
+               rg("hap", 0, 2048, "god", a, b, "R", 16 * a, 16 * b), rg("gS", 16 * a, 16 * b))
+
+    def gift_gather(e, buf, win, t, lo, hi):
+        for i, run in enumerate(runs):
+            a, b = max(lo, 10 * starts[i]), min(hi, 10 * starts[i + 1])
+            o = 10 * (G - 1) * starts[i] + 10 * t * len(run)
+            gather(e, buf, 16 * a, win, A, "goff", o + a, o + b)
+
+    def gifts(k, t, ci):
         win, buf, sent = "%s%d" % (k, t), "g" + k, "sent" + k
-        o, total, ar = 70 * t, 0, T.sem["ar" + win]
-        for ci, call in enumerate(calls[win]):
-            lo, hi = 10 * call[0][0], 10 * (call[-1][0] + 1)
-            mid = lo + 2 * int(round((hi - lo) * VSH[k] / 2))
-            gather("v", buf, 16 * lo, win, A, "goff", o + lo, o + mid)
-            gather("a", buf, 16 * mid, win, A, "goff", o + mid, o + hi)
-            tr = []
-            for pos, d, dest, h, m in call:
-                rid, pid = topo.addr(dest if h is None else h, core)
-                at = A + SG * d if h is None else 0
-                tr.append(RemoteDMATransfer(dst_ids=[DstId(rid=rid, pnc=pid)], dma_engine_mask=m, remote_sem=ar,
-                                            src=T[buf][:, SG * pos:SG * (pos + 1)], dst=T[win][:, at:at + SG]))
-                total += ones(m)
+        call, ar = calls[win][ci], T.sem["ar" + win]
+        lo, hi = 10 * call[0][0], 10 * (call[-1][0] + 1)
+        mid = lo + 2 * int(round((hi - lo) * VSH[win] / 2))
+        if win == "S0" and ci == 0:
+            first_sums(lo, hi)
+        else:
+            gift_gather("v", buf, win, t, lo, mid)
+            gift_gather("a", buf, win, t, mid, hi)
+        tr = []
+        for pos, d, dest, h, m in call:
+            rid, pid = topo.addr(dest if h is None else h, core)
+            at = A + SG * d if h is None else 0
+            tr.append(RemoteDMATransfer(dst_ids=[DstId(rid=rid, pnc=pid)], dma_engine_mask=m, remote_sem=ar,
+                                        src=T[buf][:, SG * pos:SG * (pos + 1)], dst=T[win][:, at:at + SG]))
 
-            def fn():
-                g.remote_dma_fused(tr, local_sem=T.sem[sent])
-            if ci + 1 < len(calls[win]):
-                op("g", fn, rg(buf, 16 * lo, 16 * hi), [], mark=False)
-            else:
-                op("g", fn, rg(buf, 0, 1120), [], sem=sent, inc=total)
+        def fn():
+            g.remote_dma_fused(tr, local_sem=T.sem[sent])
+        if ci + 1 < len(calls[win]):
+            op("g", fn, rg(buf, 16 * lo, 16 * hi), [], mark=False)
+        else:
+            op("g", fn, rg(buf, 0, 1120), [], sem=sent, inc=sum(ones(x[4]) for c in calls[win] for x in c))
 
-    def cross(src, o, ci, co):
-        ts(T.ta[:], T[src][:, o:o + 192], 181.0, T.cols[:, 1:2], OP.mult, OP.add, rg(src, o, o + 192, "cols", 1, 2), rg("ta", 0, 192))
+    def cross(src, ci, ti, tj, lo, hi):
+        n = hi - lo
+        ts(T.pv1[:, 0:n], T[src][:, lo:hi], 181.0, T.cols[:, 1:2], OP.mult, OP.add, rg(src, lo, hi, "cols", 1, 2), rg("pv1", 0, n))
         yield
-        tt(T.ti[:], T.ta[:], T[ci][:, co:co + 192], OP.add, rg("ta", 0, 192, ci, co, co + 192), rg("ti", 0, 192))
+        tt(T[ti][:, lo:hi], T.pv1[:, 0:n], T[ci][:, lo:hi], OP.add, rg("pv1", 0, n, ci, lo, hi), rg(ti, lo, hi))
         yield
-        ts(T.tj[:], T.ti[:], 5, 31, OP.logical_shift_right, OP.bitwise_and, rg("ti", 0, 192), rg("tj", 0, 192))
+        ts(T[tj][:, lo:hi], T[ti][:, lo:hi], 5, 31, OP.logical_shift_right, OP.bitwise_and, rg(ti, lo, hi), rg(tj, lo, hi))
         yield
 
     def dam_lists():
+        yield from cross("dl", "cid", "di", "dj", 0, 192)
+        cp("v", T.dz[:], T.dj[:], rg("dj", 0, 192), rg("dz", 0, 192))
+        yield
         cp("v", T.doff[:], T.dl[:], rg("dl", 0, 192), rg("doff", 0, 192))
         yield
-        yield from cross("dl", 0, "cid", 0)
-        cp("v", T.dz[:], T.tj[:], rg("tj", 0, 192), rg("dz", 0, 192))
+
+    def sort_rivals():
+        a, b, c = (T.rl[:, :, k, :] for k in range(3))
+        rr, hi, lo = rg("rl", 0, 576), T.pv0[:, 0:192], T.pv0[:, 192:384]
+        tt(hi, a, b, OP.max, rr, rg("pv0", 0, 192))
+        yield
+        tt(lo, a, b, OP.min, rr, rg("pv0", 192, 384))
+        yield
+        tt(T.tb[:], hi, c, OP.min, rr + rg("pv0", 0, 192), rg("tb", 0, 192))
+        tt(T.rs[:, 0:576:3], hi, c, OP.max, rr + rg("pv0", 0, 192), rg("rs", 0, 1))
+        yield
+        tt(T.rs[:, 2:576:3], lo, c, OP.min, rr + rg("pv0", 192, 384), rg("rs", 2, 3))
+        tt(T.rs[:, 1:576:3], lo, T.tb[:], OP.max, rg("pv0", 192, 384, "tb", 0, 192), rg("rs", 1, 2, "rs", 3, 576))
         yield
 
-    def sort_rivals(t):
-        o = 192 * t
-        a, b, c = (T.rl[:, o + 64 * k:o + 64 * (k + 1)] for k in range(3))
-        rr = rg("rl", o, o + 192)
-        tt(T.tb[:, 0:64], a, b, OP.max, rr, rg("tb", 0, 64))
-        yield
-        tt(T.tb[:, 64:128], a, b, OP.min, rr, rg("tb", 64, 128))
-        yield
-        tt(T.tb[:, 128:192], T.tb[:, 0:64], c, OP.min, rr + rg("tb", 0, 64), rg("tb", 128, 192))
-        yield
-        tt(T.rs[:, o:o + 192:3], T.tb[:, 0:64], c, OP.max, rr + rg("tb", 0, 64), rg("rs", o, o + 1))
-        tt(T.rs[:, o + 2:o + 192:3], T.tb[:, 64:128], c, OP.min, rr + rg("tb", 64, 128), rg("rs", o + 2, o + 3))
-        tt(T.rs[:, o + 1:o + 192:3], T.tb[:, 64:128], T.tb[:, 128:192], OP.max, rg("tb", 64, 192),
-           rg("rs", o + 1, o + 2, "rs", o + 3, o + 192))
-        yield
-        cp("v", T.roff[:, o:o + 192], T.rs[:, o:o + 192], rg("rs", o, o + 192), rg("roff", o, o + 192))
-        yield
-
-    def rival_cross(t):
-        yield from cross("rs", 192 * t, "cir", 192 * t)
+    def rival_lists(t0, t1):
+        o, e = 192 * t0, 192 * t1
+        steps = cross("rs", "cir", "ti", "tj", o, e)
+        next(steps)
+        cp("v", T.roff[:, o:e], T.rs[:, o:e], rg("rs", 0, 576), rg("roff", o, e))
+        yield from steps
         for k in range(3):
-            ts(T.u2[:, k:192:3], T.tj[:, k:192:3], 32.0 * (2 - k), None, OP.add, None, rg("tj", 0, 192),
-               rg("u2", k, k + 1) if k != 1 else rg("u2", 1, 2, "u2", 3, 192))
+            ts(T.u2[:, o + k:e:3], T.tj[:, o + k:e:3], 32.0 * (2 - k), None, OP.add, None, rg("tj", o, e),
+               rg("u2", o + k, o + k + 1) if k != 1 else rg("u2", o + 1, o + 2, "u2", o + 3, e))
         yield
 
     def weave(*gens):
@@ -323,97 +361,100 @@ def rank_program(g, core, T, topo):
         while gens:
             gens = [x for x in gens if next(x, 1) is None]
 
-    def dam_signs(t):
-        gather("a", "sgd%d" % t, 0, "tab", 96, "dz", 64 * t, 64 * (t + 1))
+    def values(b, base, c0, c1):
+        mm(b, c0 - base, c1 - base, [(T.bm[:, 15 - q:143 - q], T.R[:, 16 * c0 + q:16 * c1:16], rg("bm", 0, 144, "R", 16 * c0, 16 * c1))
+                                     for q in range(16)])
 
-    def values(bank, base, c0, c1):
-        terms = [(T.idn[:], T.tie[:, c0 - base:c1 - base], rg("idn", 0, 128, "tie", 0, 96))]
-        for q in range(16):
-            terms.append((T.bm[:, 15 - q:143 - q], T.R[:, 16 * c0 + q:16 * c1:16], rg("bm", 0, 144, "R", 16 * c0, 16 * c1)))
-        mm(bank, c0 - base, c1 - base, terms)
+    def choose(t, h, part):
+        c0, c1 = (0, HALF[t]) if h == 0 else (HALF[t], 64)
+        b, lo, hi, n = "pv%d" % h, 3 * c0, 3 * c1, 3 * (c1 - c0)
+        pv, M, nf = T[b][:, 0:n], T.M[:, lo:hi], T.nf[:, lo:hi]
+        if part == "A":
+            scan(M, T.rst[:, 0:n], pv, OP.add, rg("rst", 0, n, b, 0, n), rg("M", lo, hi))
+        elif part == "B":
+            tt(nf, pv, M, OP.not_equal, rg(b, 0, n, "M", lo, hi), rg("nf", lo, hi))
+        elif part == "C":
+            for src, e in (("u2", 2 * lo + n), ("rs", 2 * lo)):
+                scan(T.sel[:, e:e + n], nf, T[src][:, 192 * t + lo:192 * t + hi], OP.mult, rg("nf", lo, hi, src, 0, 576), rg("sel", e, e + n))
+        else:
+            cp("v", T.so[:, 2 * c0:2 * c1], T.sel[:, 2 * lo + 2:2 * hi:3], rg("sel", 2 * lo, 2 * hi), rg("so", 2 * c0, 2 * c1))
 
-    def choose(t, h):
-        bank, o, s0 = "pv%d" % h, 192 * t + 96 * h, 64 * h
-        pv = T[bank][:, 0:96]
-        scan(T.M[:], T.rst[:], pv, OP.add, rg("rst", 0, 96, bank, 0, 96), rg("M", 0, 96))
-        tt(T.nf[:], pv, T.M[:], OP.not_equal, rg(bank, 0, 96, "M", 0, 96), rg("nf", 0, 96))
-        scan(T.sel[:, 96:192], T.nf[:], T.u2[:, 96 * h:96 * (h + 1)], OP.mult, rg("nf", 0, 96, "u2", 0, 192), rg("sel", 96, 192))
-        scan(T.sel[:, 0:96], T.nf[:], T.rs[:, o:o + 96], OP.mult, rg("nf", 0, 96, "rs", 192 * t, 192 * t + 192), rg("sel", 0, 96))
-        cp("v", T.so[:, s0:s0 + 64], T.sel[:, 2:192:3], rg("sel", 0, 192), rg("so", s0, s0 + 64))
-
-    for q in range(4):
-        mm("ps%d" % q, 0, 256, [term("idn", "hap", 512 * q, 512 * (q + 1), 2), term("idn", "hap", 512 * q + 1, 512 * (q + 1), 2)])
-    for h in range(2):
-        mm("pd%d" % h, 0, 512, [term("idn", "hap", 1024 * h, 1024 * (h + 1), 2), term("nid", "hap", 1024 * h + 1, 1024 * (h + 1), 2)])
-    for q, e in ((0, "a"), (1, "v"), (2, "a"), (3, "v")):
-        cp(e, T.S0[:, 256 * q:256 * (q + 1)], T["ps%d" % q][:, 0:256], rg("ps%d" % q, 0, 256), rg("S0", 256 * q, 256 * (q + 1)), add=-255.0)
-    gift_lists(0)
-
-    for t in range(G):
-        Sw, Dw, last = "S%d" % t, "D%d" % t, t == G - 1
-        gifts("S", t)
-        for h, e in ((0, "a"), (1, "v")):
-            cp(e, T[Dw][:, 512 * h:512 * (h + 1)], T["pd%d" % h][:], rg("pd%d" % h, 0, 512), rg(Dw, 512 * h, 512 * (h + 1)))
-        gifts("D", t)
-        if t == 0:
+    def step(t, w):
+        Sw, Dw, nS, last = "S%d" % t, "D%d" % t, "S%d" % (t + 1), t == G - 1
+        if w[0] == "L":
+            lists = {"gift": gift_lists, "dam": dam_lists, "sort": sort_rivals}
+            weave(*[lists[x]() if x in lists else rival_lists(int(x[1]), int(x[-1]) + 1) for x in w[2:].split(",")])
+        elif w == "E":
             cp("v", T.cols[:, 2:3], T.ef[:, 0:1], rg("ef", 0, 1), rg("cols", 2, 3))
-            weave(dam_lists(), sort_rivals(0))
             ts(T.bm[:, 15:143:16], T.jb[:], T.cols[:, 0:1], T.cols[:, 2:3], OP.is_equal, OP.mult,
                rg("jb", 0, 8, "cols", 0, 3), rg("bm", 0, 144))
-        gather("a", "Sd", 0, Sw, A, "doff", 64 * t, 64 * (t + 1))
-        if t == 0:
-            dam_signs(0)
-        else:
-            gather("v", "Xd", 0, Dw, A, "doff", 64 * t, 64 * (t + 1), times="sgd%d" % t)
-        weave(rival_cross(t), *[sort_rivals(u) for u in range(t + 1, G) if SORT_AT[u] == t])
-        if t == 0:
-            gather("v", "Xd", 0, Dw, A, "doff", 0, 64, times="sgd0")
-        if not last:
-            gift_lists(t + 1)
-            for u in range(t + 1, G):
-                if SIGN_AT[u] == t:
-                    dam_signs(u)
-            for q in range(4):
-                mm("ps%d" % q, 0, 256, [term("hid", "Sd", 256 * q, 256 * (q + 1)), term("hid", "Xd", 256 * q, 256 * (q + 1))], last=False)
-            for h in range(2):
-                mm("pd%d" % h, 0, 512, [term("idn", "Sd", 512 * h, 512 * (h + 1)), term("idn", "Xd", 512 * h, 512 * (h + 1))], last=False)
-        else:
-            for h in range(2):
-                mm("pd%d" % h, 0, 512, [term("hid", "Sd", 512 * h, 512 * (h + 1)), term("hid", "Xd", 512 * h, 512 * (h + 1))])
-                cp(Y0[h], T.hap[:, 1024 * h:1024 * (h + 1):2], T["pd%d" % h][:], rg("pd%d" % h, 0, 512),
-                   rg("hap", 1024 * h, 1024 * (h + 1)), add=127.5)
-        o = 192 * t
-        for w in (TAIL_LAST if last else TAIL).split():
-            if ":" in w:
-                e, c0, c1 = w.split(":")
-                c0, c1 = int(c0), int(c1)
-                if e == "p":
-                    values("pv%d" % (c0 // 96), 96 * (c0 // 96), c0, c1)
-                else:
-                    gather(e, "R", 16 * c0, Sw, W, "roff", o + c0, o + c1)
-                continue
-            q = int(w[-1])
-            c, lo, hi, b = 64 * (q // 2) + 16 * (q % 2), 256 * q, 256 * (q + 1), "ps%d" % q
-            if w[0] == "c":
-                choose(t, q)
-            elif w[0] == "g":
-                gather("a", "sgs", lo, "tab", 96, "so", c + 32, c + 48)
-            elif w[0] == "s":
-                gather(w[1], "Ss", lo, Sw, W, "so", c, c + 16)
-            elif w[0] == "x":
-                gather("v", "Xs", lo, Dw, W, "so", c, c + 16, times="sgs")
-            elif w[0] == "m":
-                mm(b, 0, 256, [term("hid", "Ss", lo, hi), term("hid", "Xs", lo, hi)], first=last)
-            elif last:
-                cp(w[1], T.hap[:, 2 * lo + 1:2 * hi:2], T[b][:, 0:256], rg(b, 0, 256), rg("hap", 2 * lo, 2 * hi), add=127.5)
-                dma("s", T.y[:, 2 * lo:2 * hi], T.hap[:, 2 * lo:2 * hi], rg("hap", 2 * lo, 2 * hi), [], "st")
+        elif w[0] == "G":
+            gifts(w[1], t, int(w[2]))
+        elif w[0] in "ABCD":
+            choose(t, int(w[1]), w[0])
+        elif ":" in w:
+            e, c0, c1 = w.split(":")
+            c0, c1 = int(c0), int(c1)
+            if e == "p":
+                h = c0 >= 3 * HALF[t]
+                values("pv%d" % h, 3 * HALF[t] * h, c0, c1)
+            elif e[0] == "r":
+                gather(e[1], "R", 16 * c0, Sw, W, "roff", 192 * t + c0, 192 * t + c1)
+            elif e[0] == "S":
+                gather(e[1], "Sd", 16 * c0, Sw, A, "doff", 64 * t + c0, 64 * t + c1)
+            elif e[0] == "X":
+                gather("v", "Xd", 16 * c0, Dw, A, "doff", 64 * t + c0, 64 * t + c1, times="sgd%d" % t)
+            elif e[0] == "z":
+                gather(e[1], "sgd" + e[2], 16 * c0, "tab", 96, "dz", 64 * int(e[2]) + c0, 64 * int(e[2]) + c1)
             else:
-                n = "S%d" % (t + 1)
-                cp(w[1], T[n][:, lo:hi], T[b][:, 0:256], rg(b, 0, 256), rg(n, lo, hi))
-        if not last:
-            n = "S%d" % (t + 1)
-            for h in range(2):
-                mm("pd%d" % h, 0, 512, [term("nid", n, 512 * h, 512 * (h + 1))], first=False)
+                p, z = (0, HALF[t]) if c0 < HALF[t] else (HALF[t], 64)
+                if e[0] == "g":
+                    gather(e[1], "sgs", 16 * c0, "tab", 96, "so", z + c0, z + c1)
+                elif e[0] == "s":
+                    gather(e[1], "Ss", 16 * c0, Sw, W, "so", p + c0, p + c1)
+                else:
+                    gather("v", "Xs", 16 * c0, Dw, W, "so", p + c0, p + c1, times="sgs")
+        elif w[0] in "deNyn":
+            h = int(w[-1])
+            lo, hi, b = 512 * h, 512 * (h + 1), "pd%d" % h
+            if w[0] == "d":
+                cp(w[1], T[Dw][:, lo:hi], T[b][:], rg(b, 0, 512), rg(Dw, lo, hi))
+            elif w[0] == "e":
+                cp(w[1], T.S0[:, lo:hi], T["ps%d" % h][:], rg("ps%d" % h, 0, 512), rg("S0", lo, hi), add=-255.0)
+            elif w[0] == "N":
+                mm(b, 0, 512, [term("hid" if last else "idn", "Sd", lo, hi), term("idn" if last else "two", "Xd", lo, hi)], last=last)
+            elif w[0] == "n":
+                mm(b, 0, 512, [term("nid", nS, lo, hi)], first=False)
+            else:
+                cp(w[1], T.hap[:, 2 * lo:2 * hi:2], T[b][:], rg(b, 0, 512), rg("hap", 2 * lo, 2 * hi), add=127.5)
+        else:
+            q = int(w[-1])
+            lo, hi, b = 16 * PIECES[t][q], 16 * PIECES[t][q + 1], "ps%d" % q
+            n = hi - lo
+            out, wr = (T.hap[:, 2 * lo + 1:2 * hi:2], rg("hap", 2 * lo, 2 * hi)) if last else (T[nS][:, lo:hi], rg(nS, lo, hi))
+            if w[0] == "M":
+                mm(b, 0, n, [term("hid", "Sd", lo, hi), term("idn", "Xd", lo, hi)], last=False)
+            elif w[0] == "m":
+                if "K%d" % q not in STEPS[t]:
+                    mm(b, 0, n, [term("hid", "Ss", lo, hi), term("idn", "Xs", lo, hi)], first=last)
+                else:
+                    mm(b, 0, n, ([term("idn", "mid", 0, n)] if last else []) + [term("hid", "Ss", lo, hi)], first=last)
+            else:
+                if w[0] == "K":
+                    tt(out, T[b][:, 0:n], T.Xs[:, lo:hi], OP.add, rg(b, 0, n, "Xs", lo, hi), wr)
+                else:
+                    cp(w[1], out, T[b][:, 0:n], rg(b, 0, n), wr, add=127.5 if last else None)
+                if last:
+                    dma("s", T.y[:, 2 * lo:2 * hi], T.hap[:, 2 * lo:2 * hi], wr, [], "st")
+
+    for b, m in (("ps", "idn"), ("pd", "nid")):
+        for h in range(2):
+            mm(b + str(h), 0, 512, [term("idn", "hap", 1024 * h, 1024 * (h + 1), 2), term(m, "hap", 1024 * h + 1, 1024 * (h + 1), 2)])
+    first_lists()
+
+    for t in range(G):
+        for w in STEPS[t].split():
+            step(t + (w[0] == "+") - (w[0] == "-"), w.lstrip("+-"))
 
     for s in sorted(cnt, key=lambda s: s == "st"):
         wait("g", (s, cnt[s]))

@@ -4,36 +4,71 @@ from concourse.mybir import AluOpType, ActivationFunctionType
 A, SG, G, W = 1024, 160, 3, 2144
 BF, F32, I32, U16 = "bfloat16", "float32", "int32", "uint16"
 SCRATCH = {}
-for _d, _l in ((BF, "hap:2048 iot:128 idn:128 nid:128 hid:128 two:128 mid:512 ef:16 bm:144 tab:96 gS:1120 gD:1120 R:3072 "
-                    "sgd0:1024 sgd1:1024 sgd2:1024 Sd:1024 Xd:1024 sgs:1024 Ss:1024 Xs:1024 "
+for _d, _l in ((BF, "hap:2048 iot:128 idn:128 nid:128 hid:128 nhd:128 tbd:32 Nd:1024 mid:512 ef:16 bm:144 tab:96 wl:384 wm:768 mix:512 far:128 off:128 "
+                    "gS:1120 gD:1120 R:3072 ntw:128 sgd0:1024 sgd1:1024 sgd2:1024 Xd:1024 Sd:1024 sgs:1024 Ss:1024 Xs:1024 "
                     "S0:2144 S1:2144 S2:2144 D0:2144 D1:2144 D2:2144"),
-               (F32, "rs:576 u2:576 tb:192 cid:192 cir:576 cols:8 jb:8 zz:96 za:96 kk:144 rst:144 M:192 nf:192 sel:384"),
-               (I32, "dl:192 ti:576 tj:576 di:192 dj:192 pc:8"),
+               (F32, "f181:128 fid:128 rs:576 u2:576 tb:192 cid:192 cir:576 cols:8 jb:8 zz:96 za:96 kk:192 rst:144 M:192 nf:192 sel:384"),
+               (I32, "g0:16 dl:192 ti:576 tj:576 di:192 dc:192 ds:192 pc:8"),
                (U16, "goff:210 gev:70 god:70 doff:192 dz:192 roff:576 so:128")):
     for _x in _l.split():
         SCRATCH[_x.split(":")[0]] = ("sbuf", [128, int(_x.split(":")[1])], _d)
 SCRATCH["gl"] = ("sbuf", [128, G, 7, 10], I32)
 SCRATCH["rl"] = ("sbuf", [128, G, 3, 64], I32)
-for _n in ("pv0", "pv1", "ps0", "ps1", "ps2", "ps3", "pd0", "pd1"):
+SCRATCH["fw"] = ("sbuf", [128, 128, 16], BF)
+for _n in ("pv0", "pv1", "ps0", "ps1", "ps2", "ps3", "pw0", "pw1"):
     SCRATCH[_n] = ("psum", [128, 512], F32)
 KEYS = ["%s%d" % (k, t) for t in range(G) for k in "SD"]
-SEMAPHORES = (["c_pe", "c_v", "c_a", "c_g", "l_h0", "l_h1", "l_gl", "l_dl", "l_ef", "l_rl", "st", "sentS", "sentD"]
+SEMAPHORES = (["c_pe", "c_v", "c_a", "c_g", "l_h0", "l_h1", "l_gl", "l_g0", "l_dl", "l_ef", "l_rl", "st", "sentS", "sentD", "addS", "addN"]
               + ["ar" + k for k in KEYS])
 
 CALLS = {k: [(3, 0, k[0] == "S"), (0, 4, False)] for k in KEYS}
 CALLS["S0"] = [(0, 1, False), (0, 2, False), (0, 4, False)]
-VSH = {"S0": 0.6, "D0": 0.4, "S1": 0.5, "D1": 0.5, "S2": 0.5, "D2": 0.3}
+VSH = {"S0": 0.6, "D0": 0.3, "S1": 0.5, "D1": 0.5, "S2": 0.5, "D2": 0.3}
 LOADS = "s:h0 a:gl a:h1 s:dl s:rl s:ef"
-HALF = [30, 30, 30]
+CHOICE = [[0, 22, 44, 64]] * 3
+PIECES = [[0, 22, 44, 56, 64]] * 3
+RBANK = ["ps", "pw", "pw"]
+DIAG = {"idn": 1.0, "nid": -1.0, "ntw": -2.0, "hid": 0.5, "nhd": -0.5, "f181": 181.0, "fid": 1.0}
+RAMP = False
+CHAIN = False
+KC = ("pv0", 128, 320)
+DAMS = " Sa:0:32 X:0:32 M0 Sa:32:64 X:32:64 M1 M2 M3 "
+RIVALS = " rv:0:32 ra:32:66 p:0:66 rv:66:108 ra:108:132 p:66:132 ra:140:192 A0 B0 C0 D0 rv:132:140 p:132:192"
+SIRES = (" N0 N1 A1 B1 C1 D1 ga:0:22 ga:22:44 x:0:22 sa:0:22 A2 B2 C2 D2"
+         " sa:22:44 m0 x:22:44 m1 ga:44:64 sa:44:64 x:44:56 m2 ka0 x:56:64 ka1 K2 m3 kv3 n0 n1")
+STEPS = ["k:idn k:herd k:nid k:diff k:pc k:za k:tab L:first,gift k:rst k:fill k:ntw k:mid"
+         " ev0 GS0 ea1 GS1 GS2 L:dam da0 da1 GD0 GD1 za:0:64 L:s02 E" + DAMS + "L:xv0 +za:0:64" + RIVALS + SIRES,
+         "GS0 GS1 da0 dv1 GD0 GD1" + DAMS + "L:xv1 +za:0:64" + RIVALS + SIRES,
+         "GS0 GS1 da0 dv1 GD0 GD1 Sa:0:32 X:0:32 N0 Sa:32:64 X:32:64 N1 L:xv2 ya0 ya1" + RIVALS +
+         " A1 B1 C1 D1 ga:0:22 sa:0:22 x:0:22 m0 ga:22:44 A2 B2 C2 D2"
+         " sa:22:44 ka0 x:22:44 m1 ga:44:64 sa:44:64 x:44:56 m2 ka1 K2 m3 x:56:64 K3"]
+CHOICE = [[0, 30, 64]] * 3
 PIECES = [[0, 8, 30, 56, 64], [0, 8, 30, 56, 64], [0, 16, 30, 50, 64]]
 DAMS = " Sa:0:32 X:0:32 M0 M1 Sa:32:64 X:32:64 M2 M3 "
-HERE = (" rv:0:44 ra:44:90 p:0:90 rv:90:136 ra:136:192 za%d:44:64 A0 B0 C0 D0 p:90:192 N0 N1 A1 B1 C1 D1 ga:0:30 sa:0:30 x:0:30"
+HERE = (" rv:0:44 ra:44:90 p:0:90 rv:90:136 ra:136:192 A0 B0 C0 D0 p:90:192 N0 N1 A1 B1 C1 D1 ga:0:30 sa:0:30 x:0:30"
         " ga:42:64 gv:30:42 sa:30:58 m0 m1 x:42:64 x:30:42 sa:58:64 m2 K0 ka1 m3 ka3 K2 n0 n1")
-STEPS = ["L:gift ev0 GS0 ea1 GS1 GS2 L:dam da0 da1 E GD0 za0:0:64 L:sort" + DAMS + "L:x0 GD1 za1:0:44" + HERE % 1,
-         "GS0 GS1 da0 dv1 GD0" + DAMS + "GD1 L:x1 za2:0:44" + HERE % 2,
-         "GS0 GS1 da0 dv1 GD0 Sa:0:32 X:0:32 N0 Sa:32:64 X:32:64 N1 GD1 L:x2 ya1"
-         " rv:0:46 ra:46:90 rv:90:136 ra:136:192 p:0:90 ya0 A0 B0 C0 D0 ga:0:30 p:90:192 A1 B1 sa:0:30 C1 D1 ga:30:50 x:0:30"
+STEPS = ["k:idn k:herd k:nid k:diff k:pc k:za k:tab L:first,gift k:rst k:fill k:ntw k:mid"
+         " ev0 GS0 ea1 GS1 GS2 L:dam da0 da1 GD0 GD1 za:0:64 L:s02 E" + DAMS + "L:xv0 +za:0:64" + HERE,
+         "GS0 GS1 da0 dv1 GD0 GD1" + DAMS + "L:xv1 +za:0:64" + HERE,
+         "GS0 GS1 da0 dv1 GD0 GD1 Sa:0:32 X:0:32 N0 Sa:32:64 X:32:64 N1 L:xv2 ya0 ya1"
+         " rv:0:46 ra:46:90 rv:90:136 ra:136:192 p:0:90 A0 B0 C0 D0 ga:0:30 p:90:192 A1 B1 sa:0:30 C1 D1 ga:30:50 x:0:30"
          " m0 sa:30:50 m1 m2 K0 x:30:50 ka1 gv:50:64 sa:50:64 K2 x:50:64 m3 K3"]
+VSH = None
+PIECES = [[0, 6, 30, 58, 64], [0, 6, 30, 58, 64], [0, 16, 30, 50, 64]]
+STEPS = [
+ 'k:idn k:nid k:herd k:pc k:za k:tab l:first l:gift k:diff l:first l:gift k:rst k:fill k:ntw k:f181 k:fid GS0 ev0 ea1 l:dam l:dam l:dam l:s0 l:s0 l:dam l:s0 iv:10:30 GS1 da1 da0 l:s0 l:dam iv:30:70 GS2 jv:0:30 GD0 l:s0 l:s0 za:0:64 l:xp0 Sa:0:40 Sa:40:64 jv:30:40 E ja:40:70 GD1 X:0:44 M0 M1 l:xp0 l:xp0 X:44:64 rv:0:44 ra:44:90 l:xp0 M3 rv:90:140 ra:140:192 p:0:90 +za:0:64 l:xp0 A0 l:s1 B0 l:s1 l:s1 M2 C0 p:90:192 l:s1 D0 l:s1 N0 l:s1 l:xp1 N1 A1 B1 l:xp1 ga:0:30 C1 sa:0:30 D1 x:0:30 ga:40:64 sa:30:58 gv:30:40 m0 m1 x:52:64 ka1 sv:58:64 m2 x:30:52 K0 K2 m3 ka3 n0 n1',
+ 'iv:0:16 ia:16:30 GS0 iv:30:52 ia:52:70 GS1 da0 dv1 l:xp1 jv:0:14 ja:14:30 GD0 X:0:42 Sa:0:30 ja:62:70 l:xp1 M0 X:42:64 l:xp1 Sa:30:64 M1 M2 jv:30:62 GD1 k:mid rv:0:44 +za:0:42 ra:44:90 p:0:90 ra:136:192 rv:90:136 p:90:192 l:s2 M3 A0 l:s2 B0 l:s2 C0 l:s2 N1 D0 l:s2 +za:42:64 ga:0:30 l:s2 N0 A1 l:xp2 B1 l:xp2 C1 D1 sa:0:30 ga:40:64 x:0:30 gv:30:40 m0 m1 sv:58:64 x:48:64 sa:30:58 x:30:48 K0 m2 ka1 m3 K2 ka3 n0 n1',
+ 'iv:0:16 ia:16:30 GS0 iv:30:52 ia:52:70 GS1 da0 dv1 ja:12:30 jv:0:12 GD0 Sa:0:38 X:0:36 X:36:64 l:xp2 l:xp2 Sa:38:64 ja:44:70 N0 l:xp2 N1 ja:30:44 GD1 yv1 rv:0:46 ra:46:92 rv:92:136 ra:136:192 p:0:90 ya0 A0 p:90:192 B0 C0 D0 A1 B1 ga:0:30 C1 D1 sa:0:30 ga:30:50 x:0:30 sa:30:50 sa:50:64 m0 x:30:50 m1 m2 K0 gv:50:64 ka1 K2 m3 x:50:64 K3',
+]
+CALLS["S1"] = CALLS["S2"] = [(1, 0, True), (1, 1, False), (0, 4, False)]
+LOADS = "a:g0 s:h0 a:h1 s:gl a:dl s:rl s:ef"
+CHOICE = [[0, 32, 64]] * 3
+PIECES = [[0, 18, 32, 56, 64], [0, 18, 32, 56, 64], [0, 16, 32, 50, 64]]
+STEPS = [
+ 'k:idn k:pc k:fill k:nid k:za k:herd k:diff l:first k:f181 l:first k:fid k:rst k:tab k:ntw k:mid GS0 ea0 ea1 l:dam l:dam l:gift l:gift l:dam l:s0 iv:10:30 GS1 l:dam l:s0 l:dam da0 l:s0 da1 iv:30:54 ia:54:70 GS2 za:0:64 jv:0:38 GD0 l:s0 l:s0 ja:38:70 GD1 l:s0 Sv:54:64 l:xp0 Sa:0:54 l:xp0 X:0:52 M1 M0 l:xp0 X:52:64 M3 l:xp0 E M2 +za:0:16 l:xp0 rv:0:24 ra:24:48 p:0:48 rv:48:72 ra:72:96 p:48:96 rv:96:120 ra:120:144 p:96:144 rv:144:168 ra:168:192 p:144:192 A0 N1 N0 B0 +za:16:64 l:s1 l:s1 C0 l:s1 D0 A1 l:s1 B1 ga:0:32 l:s1 sa:0:32 C1 l:s1 D1 ga:52:64 gv:32:52 sa:32:58 x:0:32 x:42:64 m0 m1 sa:58:64 x:32:42 K0 ka1 m2 m3 K2 n0 ka3 n1',
+ 'iv:0:10 GS0 ia:10:30 GS1 iv:30:58 ia:58:70 GS2 dv1 l:xp1 da0 ja:8:30 l:xp1 jv:0:8 GD0 l:xp1 Sa:0:64 X:0:32 l:xp1 X:32:64 ja:58:70 l:xp1 jv:30:58 GD1 M0 M1 M3 M2 +za:0:42 rv:0:24 ra:24:48 p:0:48 rv:48:72 ra:72:96 p:48:96 rv:96:120 ra:120:144 p:96:144 rv:144:164 ra:164:192 p:144:192 A0 l:s2 B0 l:s2 C0 N0 D0 l:s2 +za:42:64 ga:0:32 A1 l:s2 B1 l:s2 N1 sa:0:32 C1 l:s2 D1 x:0:32 gv:32:44 ga:44:64 sa:32:56 m0 x:38:64 x:32:38 sa:56:64 m1 m2 m3 K0 ka1 n0 ka3 K2 n1',
+ 'iv:0:10 GS0 ia:10:30 GS1 iv:30:58 ia:58:70 GS2 dv1 l:xp2 l:xp2 da0 Sa:0:32 jv:0:30 GD0 l:xp2 Sa:32:64 X:0:32 N0 l:xp2 X:32:64 N1 ja:30:70 l:xp2 GD1 yv0 rv:0:24 ra:24:48 p:0:48 rv:48:72 ra:72:96 p:48:96 rv:96:120 ra:120:144 p:96:144 rv:144:166 ra:166:192 p:144:192 ya1 A0 B0 C0 D0 ga:0:18 A1 gv:18:32 B1 C1 D1 sa:0:32 ga:32:50 sa:32:50 m0 x:0:32 K0 x:32:50 m1 sa:50:64 m2 ka1 gv:50:64 m3 K2 x:50:64 K3',
+]
 
 
 def split(engs, n):
@@ -199,27 +234,29 @@ def rank_program(g, core, T, topo):
     def scan(out, d0, d1, o0, rd, wr):
         op("v", lambda: V.tensor_tensor_scan(out, d0, d1, 0.0, o0, OP.max), rd, wr)
 
-    def cp(q, out, in_, rd, wr, add=None):
+    def cp(q, out, in_, rd, wr, add=None, times=None):
         if q == "v":
-            if add is None:
-                op("v", lambda: V.tensor_copy(out, in_), rd, wr)
-            else:
+            if times is not None:
+                ts(out, in_, times, 0.0 if add is None else add, OP.mult, OP.add, rd, wr)
+            elif add is not None:
                 ts(out, in_, add, None, OP.add, None, rd, wr)
-        elif add is None:
+            else:
+                op("v", lambda: V.tensor_copy(out, in_), rd, wr)
+        elif add is None and times is None:
             op("a", lambda: S.activation(out, in_, AF.Copy), rd, wr)
         else:
-            op("a", lambda: S.activation(out, in_, AF.Identity, bias=add), rd, wr)
+            op("a", lambda: S.activation(out, in_, AF.Identity, bias=0.0 if add is None else add, scale=times or 1.0), rd, wr)
 
-    def gather(q, dst, d0, win, wn, off, c0, c1, times=None):
+    def gather(q, dst, d0, win, wn, off, c0, c1, tile=None, add=None, times=None, how=OP.mult):
         if c1 <= c0:
             return
         n = 16 * (c1 - c0)
         src = T[win][:, 0:wn].indirect(T[off][:, c0:c1])
         rd, wr = rg(win, 0, wn, off, c0, c1), rg(dst, d0, d0 + n)
-        if times is None:
-            cp(q, T[dst][:, d0:d0 + n], src, rd, wr)
+        if tile is None:
+            cp(q, T[dst][:, d0:d0 + n], src, rd, wr, add, times)
         else:
-            tt(T[dst][:, d0:d0 + n], src, T[times][:, d0:d0 + n], OP.mult, rd + rg(times, d0, d0 + n), wr)
+            tt(T[dst][:, d0:d0 + n], src, T[tile][:, d0:d0 + n], how, rd + rg(tile, d0, d0 + n), wr)
 
     def iota(n, w, pattern, base, cm):
         op("g", lambda: g.iota(T[n][:, 0:w], pattern, base, cm, allow_small_or_imprecise_dtypes=True), [], rg(n, 0, w))
@@ -232,6 +269,7 @@ def rank_program(g, core, T, topo):
 
     loads = {"h0": (T.hap[:, 0:1024], T.haps[:, 0:1024], rg("hap", 0, 1024)), "h1": (T.hap[:, 1024:2048], T.haps[:, 1024:2048], rg("hap", 1024, 2048)),
              "gl": (T.gl[:], T.gift[:], rg("gl", 0, 210)), "rl": (T.rl[:], T.rival[:], rg("rl", 0, 576)),
+             "g0": (T.g0[:, 0:10], T.gift[:, 10 * order[0]:10 * order[0] + 10], rg("g0", 0, 10)),
              "dl": (T.dl[:], T.dam[:], rg("dl", 0, 192)), "ef": (T.ef[:, 0:1], T.eff[:], rg("ef", 0, 1))}
     for w in LOADS.split():
         q, n = w.split(":")
@@ -239,23 +277,64 @@ def rank_program(g, core, T, topo):
     iota("iot", 128, [[1, 128]], 0, -1)
     op("g", lambda: g.iota(T.pc[:, 0:1], [[1, 1]], 0, 1), [], rg("pc", 0, 1))
     iota("zz", 96, [[0, 3], [2, 32]], -17, -2)
-    iota("kk", 144, [[0, 48], [-1, 3]], 2, 0)
+    iota("kk", 192, [[0, 64], [-1, 3]], 2, 0)
     iota("jb", 8, [[32, 8]], 0, 0)
     iota("cid", 192, [[217, 3], [1200, 64]], 0, 75)
     iota("cir", 576, [[217, 3], [1200, 64], [0, 3]], 389, 75)
-    ts(T.idn[:], T.iot[:], 0.0, None, OP.is_equal, None, rg("iot", 0, 128), rg("idn", 0, 128))
-    ts(T.nid[:], T.iot[:], 0.0, -1.0, OP.is_equal, OP.mult, rg("iot", 0, 128), rg("nid", 0, 128))
-    ts(T.hid[:], T.iot[:], 0.0, 0.5, OP.is_equal, OP.mult, rg("iot", 0, 128), rg("hid", 0, 128))
-    ts(T.two[:], T.iot[:], 0.0, 2.0, OP.is_equal, OP.mult, rg("iot", 0, 128), rg("two", 0, 128))
-    op("v", lambda: V.memset(T.bm[:], 0.0), [], rg("bm", 0, 144))
-    op("v", lambda: V.memset(T.mid[:], 127.5), [], rg("mid", 0, 512))
-    ts(T.pc[:, 1:2], T.pc[:, 0:1], 112, None, OP.bitwise_and, None, rg("pc", 0, 1), rg("pc", 1, 2))
-    ts(T.cols[:, 0:1], T.pc[:, 1:2], 2.0, None, OP.mult, None, rg("pc", 1, 2), rg("cols", 0, 1))
-    ts(T.cols[:, 1:2], T.pc[:, 1:2], -75.0, None, OP.mult, None, rg("pc", 1, 2), rg("cols", 1, 2))
-    ts(T.rst[:], T.kk[:], 2.0, -4194304.0, OP.is_equal, OP.mult, rg("kk", 0, 144), rg("rst", 0, 144))
-    ts(T.rst[:], T.rst[:], 0.25, None, OP.add, None, rg("rst", 0, 144), rg("rst", 0, 144))
-    op("a", lambda: S.activation(T.za[:], T.zz[:], AF.Abs, bias=T.cols[:, 0:1]), rg("zz", 0, 96, "cols", 0, 1), rg("za", 0, 96))
-    ts(T.tab[:], T.za[:], 16.0, 0.5, OP.is_lt, OP.subtract, rg("za", 0, 96), rg("tab", 0, 96))
+
+    def diag(n, lo, at, x, rd=()):
+        ts(T[n][:, lo:lo + 128], T.iot[:], at, x, OP.is_equal, OP.mult, rg("iot", 0, 128, *rd), rg(n, lo, lo + 128))
+
+    def col(c, src, x, y):
+        ts(T.cols[:, c:c + 1], T.pc[:, src:src + 1], x, y, OP.mult, OP.add, rg("pc", src, src + 1), rg("cols", c, c + 1))
+
+    def constant(n):
+        if n in DIAG:
+            diag(n, 0, 0.0, DIAG[n])
+        elif n == "fill":
+            op("v", lambda: V.memset(T.bm[:], 0.0), [], rg("bm", 0, 144))
+        elif n == "mid":
+            op("v", lambda: V.memset(T.mid[:], 127.5), [], rg("mid", 0, 512))
+        elif n == "pc":
+            ts(T.pc[:, 1:2], T.pc[:, 0:1], 112, None, OP.bitwise_and, None, rg("pc", 0, 1), rg("pc", 1, 2))
+            col(0, 1, 2.0, 0.0)
+            col(1, 1, -75.0, 0.0)
+        elif n == "odd":
+            ts(T.pc[:, 2:3], T.pc[:, 0:1], 1, None, OP.bitwise_and, None, rg("pc", 0, 1), rg("pc", 2, 3))
+            col(3, 2, 64.0, -32.0)
+        elif n == "abs":
+            op("a", lambda: S.activation(T.off[:], T.iot[:], AF.Abs), rg("iot", 0, 128), rg("off", 0, 128))
+            op("a", lambda: S.activation(T.far[:], T.iot[:], AF.Abs, bias=T.cols[:, 3:4], scale=64.0), rg("iot", 0, 128, "cols", 3, 4), rg("far", 0, 128))
+        elif n == "za":
+            op("a", lambda: S.activation(T.za[:], T.zz[:], AF.Abs, bias=T.cols[:, 0:1]), rg("zz", 0, 96, "cols", 0, 1), rg("za", 0, 96))
+        elif n == "far":
+            tt(T.far[:], T.far[:], T.off[:], OP.add, rg("far", 0, 128, "off", 0, 128), rg("far", 0, 128))
+            ts(T.off[:], T.far[:], -1.0, 33.5, OP.mult, OP.add, rg("far", 0, 128), rg("off", 0, 128))
+        elif n[:2] == "fw":
+            for r in range(4 * int(n[3]), 4 * int(n[3]) + 4):
+                if n[2] == "a":
+                    op("a", lambda: S.activation(T.fw[:, :, r], T.off[:], AF.Relu, bias=float(r)), rg("off", 0, 128), rg("fw", r, r + 1))
+                else:
+                    ts(T.fw[:, :, r], T.off[:], float(r), 0.0, OP.add, OP.max, rg("off", 0, 128), rg("fw", r, r + 1))
+        elif n == "mix":
+            for c, x, y in ((4, -1.0, 1.0), (5, 1.0, 0.0), (6, 1.0, -1.0), (7, -1.0, 0.0)):
+                col(c, 2, x, y)
+            for i, at in enumerate((0.0, 0.0, 1.0, -1.0)):
+                diag("mix", 128 * i, at, T.cols[:, 4 + i:5 + i], ("cols", 4 + i, 5 + i))
+        elif n == "rst":
+            ts(T.rst[:], T.kk[:, 0:144], 2.0, -4194304.0, OP.is_equal, OP.mult, rg("kk", 0, 144), rg("rst", 0, 144))
+            ts(T[KC[0]][:, KC[1]:KC[2]], T.kk[:], 32.0, None, OP.mult, None, rg("kk", 0, 192), rg(*KC))
+            ts(T.rst[:], T.rst[:], 0.25, None, OP.add, None, rg("rst", 0, 144), rg("rst", 0, 144))
+        elif n == "tbd":
+            ts(T.tbd[:], T.za[:, 0:32], 16.0, -2.0, OP.is_ge, OP.mult, rg("za", 0, 96), rg("tbd", 0, 32))
+        elif n == "tab":
+            ts(T.tab[:], T.za[:], 16.0, 0.5, OP.is_ge, OP.subtract, rg("za", 0, 96), rg("tab", 0, 96))
+        elif n == "herd":
+            for h in range(2):
+                mm("ps%d" % h, 0, 512, [term("idn", "hap", 1024 * h, 1024 * (h + 1), 2), term("idn", "hap", 1024 * h + 1, 1024 * (h + 1), 2)])
+        elif n == "diff":
+            for h in range(2):
+                mm("pw%d" % h, 0, 512, [term("idn", "hap", 1024 * h + 1, 1024 * (h + 1), 2), term("nid", "hap", 1024 * h, 1024 * (h + 1), 2)])
 
     runs = []
     for d in order:
@@ -275,7 +354,11 @@ def rank_program(g, core, T, topo):
         for pos, d, dest, h, m in calls["S0"][0]:
             lo, hi = 10 * pos, 10 * (pos + 1)
             for n, s in (("gev", 0.0), ("god", 1.0)):
-                ts(T[n][:, lo:hi], T.gl[:, 0, d, :], 2.0, s, OP.mult, OP.add, rg("gl", 0, 210), rg(n, lo, hi))
+                if "g0" in LOADS:
+                    ts(T[n][:, lo:hi], T.g0[:, 0:10], 2.0, s, OP.mult, OP.add, rg("g0", 0, 10), rg(n, lo, hi))
+                else:
+                    ts(T[n][:, lo:hi], T.gl[:, 0, d, :], 2.0, s, OP.mult, OP.add, rg("gl", 0, 210), rg(n, lo, hi))
+                yield
 
     def first_sums(lo, hi):
         for a in range(lo, hi, 20):
@@ -292,68 +375,100 @@ def rank_program(g, core, T, topo):
             gather(e, buf, 16 * a, win, A, "goff", o + a, o + b)
 
     def gifts(k, t, ci):
-        win, buf, sent = "%s%d" % (k, t), "g" + k, "sent" + k
+        win, sent = "%s%d" % (k, t), "sent" + k
+        bufs = ["gS", "gD"] if CHAIN and k == "D" else ["g" + k]
         call, ar = calls[win][ci], T.sem["ar" + win]
         lo, hi = 10 * call[0][0], 10 * (call[-1][0] + 1)
-        mid = lo + 2 * int(round((hi - lo) * VSH[win] / 2))
         if win == "S0" and ci == 0:
             first_sums(lo, hi)
-        else:
-            gift_gather("v", buf, win, t, lo, mid)
-            gift_gather("a", buf, win, t, mid, hi)
+        elif VSH:
+            mid = lo + 2 * int(round((hi - lo) * VSH[win] / 2))
+            gift_gather("v", "g" + k, win, t, lo, mid)
+            gift_gather("a", "g" + k, win, t, mid, hi)
         tr = []
         for pos, d, dest, h, m in call:
             rid, pid = topo.addr(dest if h is None else h, core)
             at = A + SG * d if h is None else 0
             tr.append(RemoteDMATransfer(dst_ids=[DstId(rid=rid, pnc=pid)], dma_engine_mask=m, remote_sem=ar,
-                                        src=T[buf][:, SG * pos:SG * (pos + 1)], dst=T[win][:, at:at + SG]))
+                                        srcs=[T[b][:, SG * pos:SG * (pos + 1)] for b in bufs], dsts=[T[win][:, at:at + SG]],
+                                        alu_op=len(bufs) - 1))
 
         def fn():
             g.remote_dma_fused(tr, local_sem=T.sem[sent])
         if ci + 1 < len(calls[win]):
-            op("g", fn, rg(buf, 16 * lo, 16 * hi), [], mark=False)
+            op("g", fn, [(b, 16 * lo, 16 * hi) for b in bufs], [], mark=False)
         else:
-            op("g", fn, rg(buf, 0, 1120), [], sem=sent, inc=sum(ones(x[4]) for c in calls[win] for x in c))
+            op("g", fn, [(b, 0, 1120) for b in bufs], [], sem=sent, inc=sum(ones(x[4]) for c in calls[win] for x in c))
 
-    def cross(src, ci, ti, tj, lo, hi):
+    def cross(src, ci, ti, lo, hi, q="v"):
         n = hi - lo
-        ts(T.pv1[:, 0:n], T[src][:, lo:hi], 181.0, T.cols[:, 1:2], OP.mult, OP.add, rg(src, lo, hi, "cols", 1, 2), rg("pv1", 0, n))
+        if q == "p":
+            mm("pv0", 320, 512, [term("f181", src, lo, hi), term("fid", ci, lo, hi)])
+            yield
+            ts(T[ti][:, lo:hi], T.pv0[:, 320:512], T.cols[:, 1:2], None, OP.add, None, rg("pv0", 320, 512, "cols", 1, 2), rg(ti, lo, hi))
+            yield
+            return
+        cp(q, T.pv1[:, 0:n], T[src][:, lo:hi], rg(src, lo, hi, "cols", 1, 2), rg("pv1", 0, n), add=T.cols[:, 1:2], times=181.0)
         yield
         tt(T[ti][:, lo:hi], T.pv1[:, 0:n], T[ci][:, lo:hi], OP.add, rg("pv1", 0, n, ci, lo, hi), rg(ti, lo, hi))
         yield
-        ts(T[tj][:, lo:hi], T[ti][:, lo:hi], 5, 31, OP.logical_shift_right, OP.bitwise_and, rg(ti, lo, hi), rg(tj, lo, hi))
-        yield
+
+    def field(out, src, shift, mask, lo, hi):
+        ts(T[out][:, lo:hi], T[src][:, lo:hi], shift, mask, OP.logical_shift_right, OP.bitwise_and, rg(src, lo, hi), rg(out, lo, hi))
 
     def dam_lists():
-        yield from cross("dl", "cid", "di", "dj", 0, 192)
-        cp("v", T.dz[:], T.dj[:], rg("dj", 0, 192), rg("dz", 0, 192))
+        steps = cross("dl", "cid", "di", 0, 192)
+        next(steps)
         yield
         cp("v", T.doff[:], T.dl[:], rg("dl", 0, 192), rg("doff", 0, 192))
         yield
-
-    def sort_rivals():
-        a, b, c = (T.rl[:, :, k, :] for k in range(3))
-        rr, hi, lo = rg("rl", 0, 576), T.pv0[:, 0:192], T.pv0[:, 192:384]
-        tt(hi, a, b, OP.max, rr, rg("pv0", 0, 192))
-        yield
-        tt(lo, a, b, OP.min, rr, rg("pv0", 192, 384))
-        yield
-        tt(T.tb[:], hi, c, OP.min, rr + rg("pv0", 0, 192), rg("tb", 0, 192))
-        tt(T.rs[:, 0:576:3], hi, c, OP.max, rr + rg("pv0", 0, 192), rg("rs", 0, 1))
-        yield
-        tt(T.rs[:, 2:576:3], lo, c, OP.min, rr + rg("pv0", 192, 384), rg("rs", 2, 3))
-        tt(T.rs[:, 1:576:3], lo, T.tb[:], OP.max, rg("pv0", 192, 384, "tb", 0, 192), rg("rs", 1, 2, "rs", 3, 576))
-        yield
-
-    def rival_lists(t0, t1):
-        o, e = 192 * t0, 192 * t1
-        steps = cross("rs", "cir", "ti", "tj", o, e)
-        next(steps)
-        cp("v", T.roff[:, o:e], T.rs[:, o:e], rg("rs", 0, 576), rg("roff", o, e))
         yield from steps
-        for k in range(3):
-            ts(T.u2[:, o + k:e:3], T.tj[:, o + k:e:3], 32.0 * (2 - k), None, OP.add, None, rg("tj", o, e),
-               rg("u2", o + k, o + k + 1) if k != 1 else rg("u2", o + 1, o + 2, "u2", o + 3, e))
+        if not RAMP:
+            field("dc", "di", 5, 31, 0, 192)
+            yield
+            cp("v", T.dz[:], T.dc[:], rg("dc", 0, 192), rg("dz", 0, 192))
+            yield
+            return
+        field("ds", "di", 9, 1, 0, 192)
+        field("dc", "di", 5, 15, 0, 192)
+        sg = T.pv1[:, 0:192]
+        ts(sg, T.ds[:], -1024.0, 512.0, OP.mult, OP.add, rg("ds", 0, 192), rg("pv1", 0, 192))
+        yield
+        tt(T.wl[:, 0:192], T.dc[:], sg, OP.mult, rg("dc", 0, 192, "pv1", 0, 192), rg("wl", 0, 192))
+        yield
+        tt(T.wl[:, 192:384], T.wl[:, 0:192], sg, OP.add, rg("wl", 0, 192, "pv1", 0, 192), rg("wl", 192, 384))
+        yield
+
+    def sort_rivals(t0, t1):
+        a, b, c = (T.rl[:, t0:t1, k, :] for k in range(3))
+        n, o, e = 64 * (t1 - t0), 192 * t0, 192 * t1
+        p = 320 if n == 64 else 0
+        rh, rl = rg("pv0", p, p + n), rg("pv0", p + n, p + 2 * n)
+        rr, hi, lo, tb = rg("rl", 0, 576), T.pv0[:, p:p + n], T.pv0[:, p + n:p + 2 * n], T.tb[:, 0:n]
+        tt(hi, a, b, OP.max, rr, rh)
+        yield
+        tt(lo, a, b, OP.min, rr, rl)
+        yield
+        tt(tb, hi, c, OP.min, rr + rh, rg("tb", 0, 192))
+        yield
+        tt(T.rs[:, o:e:3], hi, c, OP.max, rr + rh, rg("rs", o, o + 1))
+        yield
+        tt(T.rs[:, o + 2:e:3], lo, c, OP.min, rr + rl, rg("rs", o + 2, o + 3))
+        yield
+        tt(T.rs[:, o + 1:e:3], lo, tb, OP.max, rl + rg("tb", 0, 192), rg("rs", o + 1, o + 2, "rs", o + 3, e))
+        yield
+
+    def rival_lists(t, q):
+        o, e = 192 * t, 192 * (t + 1)
+        steps = cross("rs", "cir", "ti", o, e, q)
+        next(steps)
+        yield
+        cp("v", T.roff[:, o:e], T.rs[:, o:e], rg("rs", o, e), rg("roff", o, e))
+        yield
+        yield from steps
+        field("tj", "ti", 5, 31, o, e)
+        yield
+        tt(T.u2[:, o:e], T.tj[:, o:e], T[KC[0]][:, KC[1]:KC[2]], OP.add, rg("tj", o, e, *KC), rg("u2", o, e))
         yield
 
     def weave(*gens):
@@ -365,9 +480,18 @@ def rank_program(g, core, T, topo):
         mm(b, c0 - base, c1 - base, [(T.bm[:, 15 - q:143 - q], T.R[:, 16 * c0 + q:16 * c1:16], rg("bm", 0, 144, "R", 16 * c0, 16 * c1))
                                      for q in range(16)])
 
+    def ramp(b, t, par):
+        o = 192 * par + 64 * t
+
+        def fn():
+            for q in range(par, 16, 2):
+                ins = g.tensor.matmul(T[b][:, q // 2:512:8], T.fw[:, q:128:16, :], T.wm[:, o:o + 64], True, True)
+            return ins
+        op("pe", fn, rg("fw", 0, 16, "wm", o, o + 64), rg(b, 0, 512))
+
     def choose(t, h, part):
-        c0, c1 = (0, HALF[t]) if h == 0 else (HALF[t], 64)
-        b, lo, hi, n = "pv%d" % h, 3 * c0, 3 * c1, 3 * (c1 - c0)
+        c0, c1 = CHOICE[t][h:h + 2]
+        b, lo, hi, n = "pv%d" % (h % 2), 3 * c0, 3 * c1, 3 * (c1 - c0)
         pv, M, nf = T[b][:, 0:n], T.M[:, lo:hi], T.nf[:, lo:hi]
         if part == "A":
             scan(M, T.rst[:, 0:n], pv, OP.add, rg("rst", 0, n, b, 0, n), rg("M", lo, hi))
@@ -375,19 +499,40 @@ def rank_program(g, core, T, topo):
             tt(nf, pv, M, OP.not_equal, rg(b, 0, n, "M", lo, hi), rg("nf", lo, hi))
         elif part == "C":
             for src, e in (("u2", 2 * lo + n), ("rs", 2 * lo)):
-                scan(T.sel[:, e:e + n], nf, T[src][:, 192 * t + lo:192 * t + hi], OP.mult, rg("nf", lo, hi, src, 0, 576), rg("sel", e, e + n))
+                scan(T.sel[:, e:e + n], nf, T[src][:, 192 * t + lo:192 * t + hi], OP.mult, rg("nf", lo, hi, src, 192 * t, 192 * t + 192), rg("sel", e, e + n))
         else:
             cp("v", T.so[:, 2 * c0:2 * c1], T.sel[:, 2 * lo + 2:2 * hi:3], rg("sel", 2 * lo, 2 * hi), rg("so", 2 * c0, 2 * c1))
 
+    running = {}
+    XW = ("hid", "nid") if RAMP else ("idn", "ntw")
+
     def step(t, w):
-        Sw, Dw, nS, last = "S%d" % t, "D%d" % t, "S%d" % (t + 1), t == G - 1
-        if w[0] == "L":
-            lists = {"gift": gift_lists, "dam": dam_lists, "sort": sort_rivals}
-            weave(*[lists[x]() if x in lists else rival_lists(int(x[1]), int(x[-1]) + 1) for x in w[2:].split(",")])
+        Sw, Dw, nS, nD, last = "S%d" % t, "D%d" % t, "S%d" % (t + 1), "D%d" % (t + 1), t == G - 1
+        nN = "Nd" if last else nD
+        if w[0] in "Ll":
+            lists = {"gift": gift_lists, "dam": dam_lists, "first": first_lists}
+            for x in w[2:].split(","):
+                if x not in running:
+                    running[x] = lists[x]() if x in lists else sort_rivals(int(x[1]), int(x[-1]) + 1) if x[0] == "s" else rival_lists(int(x[2]), x[1])
+            if w[0] == "L":
+                weave(*[running[x] for x in w[2:].split(",")])
+            else:
+                next(running[w[2:]], 1)
+        elif w[:2] == "k:":
+            for x in w[2:].split(","):
+                constant(x)
         elif w == "E":
             cp("v", T.cols[:, 2:3], T.ef[:, 0:1], rg("ef", 0, 1), rg("cols", 2, 3))
             ts(T.bm[:, 15:143:16], T.jb[:], T.cols[:, 0:1], T.cols[:, 2:3], OP.is_equal, OP.mult,
                rg("jb", 0, 8, "cols", 0, 3), rg("bm", 0, 144))
+        elif w[:3] == "mix":
+            for h in range(2):
+                mm("ps3", 192 * h, 192 * (h + 1), [(T.mix[:, 128 * (h + 2 * i):128 * (h + 2 * i + 1)], T.wl[:, 192 * i:192 * (i + 1)],
+                                                    rg("mix", 0, 512, "wl", 0, 384)) for i in range(2)])
+            cp(w[3], T.wm[:, 0:384], T.ps3[:, 0:384], rg("ps3", 0, 384), rg("wm", 0, 384))
+        elif w[:3] == "ADD":
+            to, src = (Dw, Sw) if w[3] == "S" else (nD, "Xd")
+            op("g", lambda: g.dma_start(T[to][:, 0:A], T[src][:, 0:A], accum_op=OP.add), rg(src, 0, A, to, 0, A), rg(to, 0, A), sem="add" + w[3], inc=16)
         elif w[0] == "G":
             gifts(w[1], t, int(w[2]))
         elif w[0] in "ABCD":
@@ -396,35 +541,53 @@ def rank_program(g, core, T, topo):
             e, c0, c1 = w.split(":")
             c0, c1 = int(c0), int(c1)
             if e == "p":
-                h = c0 >= 3 * HALF[t]
-                values("pv%d" % h, 3 * HALF[t] * h, c0, c1)
+                h = max(i for i, c in enumerate(CHOICE[t]) if 3 * c <= c0)
+                values("pv%d" % (h % 2), 3 * CHOICE[t][h], c0, c1)
             elif e[0] == "r":
                 gather(e[1], "R", 16 * c0, Sw, W, "roff", 192 * t + c0, 192 * t + c1)
+            elif e[0] in "ij":
+                k = "SD"[e[0] == "j"]
+                gift_gather(e[1], "g" + k, k + str(t), t, c0, c1)
             elif e[0] == "S":
-                gather(e[1], "Sd", 16 * c0, Sw, A, "doff", 64 * t + c0, 64 * t + c1)
+                gather(e[1], "Sd", 16 * c0, Sw, A, "doff", 64 * t + c0, 64 * t + c1, times=0.5)
+            elif e[0] == "a":
+                gather(e[1], nN, 16 * c0, Dw, A, "doff", 64 * t + c0, 64 * t + c1)
+            elif e[0] == "c":
+                gather("v", "Sd", 16 * c0, Sw, A, "doff", 64 * t + c0, 64 * t + c1, tile=nN, how=OP.add)
+            elif e[0] == "b":
+                gather("v", "Xd", 16 * c0, "tbd", 32, "dz", 64 * t + c0, 64 * t + c1, tile="Sd")
             elif e[0] == "X":
-                gather("v", "Xd", 16 * c0, Dw, A, "doff", 64 * t + c0, 64 * t + c1, times="sgd%d" % t)
+                gather("v", "Xd", 16 * c0, Dw, A, "doff", 64 * t + c0, 64 * t + c1, tile="sgd%d" % t)
             elif e[0] == "z":
-                gather(e[1], "sgd" + e[2], 16 * c0, "tab", 96, "dz", 64 * int(e[2]) + c0, 64 * int(e[2]) + c1)
+                gather(e[1], "sgd%d" % t, 16 * c0, "tab", 96, "dz", 64 * t + c0, 64 * t + c1)
             else:
-                p, z = (0, HALF[t]) if c0 < HALF[t] else (HALF[t], 64)
+                h = max(i for i, c in enumerate(CHOICE[t]) if c <= c0)
+                p, z = CHOICE[t][h:h + 2]
                 if e[0] == "g":
                     gather(e[1], "sgs", 16 * c0, "tab", 96, "so", z + c0, z + c1)
                 elif e[0] == "s":
-                    gather(e[1], "Ss", 16 * c0, Sw, W, "so", p + c0, p + c1)
+                    gather(e[1], "Ss", 16 * c0, Sw, W, "so", p + c0, p + c1, times=0.5)
                 else:
-                    gather("v", "Xs", 16 * c0, Dw, W, "so", p + c0, p + c1, times="sgs")
-        elif w[0] in "deNyn":
+                    gather("v", "Xs", 16 * c0, Dw, W, "so", p + c0, p + c1, tile="sgs")
+        elif w[0] in "deWYNnyH":
             h = int(w[-1])
-            lo, hi, b = 512 * h, 512 * (h + 1), "pd%d" % h
+            lo, hi, b, rb = 512 * h, 512 * (h + 1), "pw%d" % h, RBANK[t] + str(h + 2 * (RBANK[t] == "ps"))
             if w[0] == "d":
                 cp(w[1], T[Dw][:, lo:hi], T[b][:], rg(b, 0, 512), rg(Dw, lo, hi))
             elif w[0] == "e":
                 cp(w[1], T.S0[:, lo:hi], T["ps%d" % h][:], rg("ps%d" % h, 0, 512), rg("S0", lo, hi), add=-255.0)
+            elif w[0] == "W":
+                ramp(rb, t, h)
+            elif w[0] == "Y":
+                op("a", lambda: S.activation(T["sgd%d" % t][:, h:A:2], T[rb][:], AF.Sign, scale=-1.0), rg(rb, 0, 512), rg("sgd%d" % t, h, A if h else 1))
+            elif w[0] == "H":
+                cp(w[1], T.D0[:, lo:hi], T.hap[:, 2 * lo:2 * hi:2], rg("hap", 2 * lo, 2 * hi), rg("D0", lo, hi), add=255.0, times=-2.0)
+            elif w[0] == "N" and CHAIN:
+                mm(b, 0, 512, [term("nhd", nN, lo, hi), term("nhd", "Xd", lo, hi)])
             elif w[0] == "N":
-                mm(b, 0, 512, [term("hid" if last else "idn", "Sd", lo, hi), term("idn" if last else "two", "Xd", lo, hi)], last=last)
+                mm(b, 0, 512, [term("idn" if last else "ntw", "Sd", lo, hi), term(XW[0] if last else XW[1], "Xd", lo, hi)], last=last)
             elif w[0] == "n":
-                mm(b, 0, 512, [term("nid", nS, lo, hi)], first=False)
+                mm(b, 0, 512, [term("idn", nS, lo, hi)], first=False)
             else:
                 cp(w[1], T.hap[:, 2 * lo:2 * hi:2], T[b][:], rg(b, 0, 512), rg("hap", 2 * lo, 2 * hi), add=127.5)
         else:
@@ -432,13 +595,15 @@ def rank_program(g, core, T, topo):
             lo, hi, b = 16 * PIECES[t][q], 16 * PIECES[t][q + 1], "ps%d" % q
             n = hi - lo
             out, wr = (T.hap[:, 2 * lo + 1:2 * hi:2], rg("hap", 2 * lo, 2 * hi)) if last else (T[nS][:, lo:hi], rg(nS, lo, hi))
-            if w[0] == "M":
-                mm(b, 0, n, [term("hid", "Sd", lo, hi), term("idn", "Xd", lo, hi)], last=False)
+            if w[0] == "M" and CHAIN:
+                mm(b, 0, n, [term("nhd", nN, lo, hi), term("nhd", "Xd", lo, hi)], last=False)
+            elif w[0] == "M":
+                mm(b, 0, n, [term("idn", "Sd", lo, hi), term(XW[0], "Xd", lo, hi)], last=False)
             elif w[0] == "m":
                 if "K%d" % q not in STEPS[t]:
-                    mm(b, 0, n, [term("hid", "Ss", lo, hi), term("idn", "Xs", lo, hi)], first=last)
+                    mm(b, 0, n, [term("idn", "Ss", lo, hi), term("idn", "Xs", lo, hi)], first=last)
                 else:
-                    mm(b, 0, n, ([term("idn", "mid", 0, n)] if last else []) + [term("hid", "Ss", lo, hi)], first=last)
+                    mm(b, 0, n, ([term("idn", "mid", 0, n)] if last else []) + [term("idn", "Ss", lo, hi)], first=last)
             else:
                 if w[0] == "K":
                     tt(out, T[b][:, 0:n], T.Xs[:, lo:hi], OP.add, rg(b, 0, n, "Xs", lo, hi), wr)
@@ -446,11 +611,6 @@ def rank_program(g, core, T, topo):
                     cp(w[1], out, T[b][:, 0:n], rg(b, 0, n), wr, add=127.5 if last else None)
                 if last:
                     dma("s", T.y[:, 2 * lo:2 * hi], T.hap[:, 2 * lo:2 * hi], wr, [], "st")
-
-    for b, m in (("ps", "idn"), ("pd", "nid")):
-        for h in range(2):
-            mm(b + str(h), 0, 512, [term("idn", "hap", 1024 * h, 1024 * (h + 1), 2), term(m, "hap", 1024 * h + 1, 1024 * (h + 1), 2)])
-    first_lists()
 
     for t in range(G):
         for w in STEPS[t].split():

from concourse.bass import DstId, RemoteDMATransfer
from concourse.mybir import AluOpType, ActivationFunctionType

A, SG, G, W = 1024, 160, 3, 2144
BF, F32, I32, U16 = "bfloat16", "float32", "int32", "uint16"
SCRATCH = {}
for _d, _l in ((BF, "hap:2048 iot:128 idn:128 nid:128 hid:128 nhd:128 tbd:32 Nd:1024 mid:512 ef:16 bm:144 tab:96 wl:384 wm:768 mix:512 far:128 off:128 "
                    "gS:1120 gD:1120 R:3072 ntw:128 sgd0:1024 sgd1:1024 sgd2:1024 Xd:1024 Sd:1024 sgs:1024 Ss:1024 Xs:1024 "
                    "S0:2144 S1:2144 S2:2144 D0:2144 D1:2144 D2:2144"),
               (F32, "f181:128 fid:128 rs:576 u2:576 tb:192 cid:192 cir:576 cols:8 jb:8 zz:96 za:96 kk:192 rst:144 M:192 nf:192 sel:384"),
               (I32, "g0:16 dl:192 ti:576 tj:576 di:192 dc:192 ds:192 pc:8"),
               (U16, "goff:210 gev:70 god:70 doff:192 dz:192 roff:576 so:128")):
    for _x in _l.split():
        SCRATCH[_x.split(":")[0]] = ("sbuf", [128, int(_x.split(":")[1])], _d)
SCRATCH["gl"] = ("sbuf", [128, G, 7, 10], I32)
SCRATCH["rl"] = ("sbuf", [128, G, 3, 64], I32)
SCRATCH["fw"] = ("sbuf", [128, 128, 16], BF)
for _n in ("pv0", "pv1", "ps0", "ps1", "ps2", "ps3", "pw0", "pw1"):
    SCRATCH[_n] = ("psum", [128, 512], F32)
KEYS = ["%s%d" % (k, t) for t in range(G) for k in "SD"]
SEMAPHORES = (["c_pe", "c_v", "c_a", "c_g", "l_h0", "l_h1", "l_gl", "l_g0", "l_dl", "l_ef", "l_rl", "st", "sentS", "sentD", "addS", "addN"]
              + ["ar" + k for k in KEYS])

CALLS = {k: [(3, 0, k[0] == "S"), (0, 4, False)] for k in KEYS}
CALLS["S0"] = [(0, 1, False), (0, 2, False), (0, 4, False)]
VSH = {"S0": 0.6, "D0": 0.3, "S1": 0.5, "D1": 0.5, "S2": 0.5, "D2": 0.3}
LOADS = "s:h0 a:gl a:h1 s:dl s:rl s:ef"
CHOICE = [[0, 22, 44, 64]] * 3
PIECES = [[0, 22, 44, 56, 64]] * 3
RBANK = ["ps", "pw", "pw"]
DIAG = {"idn": 1.0, "nid": -1.0, "ntw": -2.0, "hid": 0.5, "nhd": -0.5, "f181": 181.0, "fid": 1.0}
RAMP = False
CHAIN = False
KC = ("pv0", 128, 320)
DAMS = " Sa:0:32 X:0:32 M0 Sa:32:64 X:32:64 M1 M2 M3 "
RIVALS = " rv:0:32 ra:32:66 p:0:66 rv:66:108 ra:108:132 p:66:132 ra:140:192 A0 B0 C0 D0 rv:132:140 p:132:192"
SIRES = (" N0 N1 A1 B1 C1 D1 ga:0:22 ga:22:44 x:0:22 sa:0:22 A2 B2 C2 D2"
         " sa:22:44 m0 x:22:44 m1 ga:44:64 sa:44:64 x:44:56 m2 ka0 x:56:64 ka1 K2 m3 kv3 n0 n1")
STEPS = ["k:idn k:herd k:nid k:diff k:pc k:za k:tab L:first,gift k:rst k:fill k:ntw k:mid"
         " ev0 GS0 ea1 GS1 GS2 L:dam da0 da1 GD0 GD1 za:0:64 L:s02 E" + DAMS + "L:xv0 +za:0:64" + RIVALS + SIRES,
         "GS0 GS1 da0 dv1 GD0 GD1" + DAMS + "L:xv1 +za:0:64" + RIVALS + SIRES,
         "GS0 GS1 da0 dv1 GD0 GD1 Sa:0:32 X:0:32 N0 Sa:32:64 X:32:64 N1 L:xv2 ya0 ya1" + RIVALS +
         " A1 B1 C1 D1 ga:0:22 sa:0:22 x:0:22 m0 ga:22:44 A2 B2 C2 D2"
         " sa:22:44 ka0 x:22:44 m1 ga:44:64 sa:44:64 x:44:56 m2 ka1 K2 m3 x:56:64 K3"]
CHOICE = [[0, 30, 64]] * 3
PIECES = [[0, 8, 30, 56, 64], [0, 8, 30, 56, 64], [0, 16, 30, 50, 64]]
DAMS = " Sa:0:32 X:0:32 M0 M1 Sa:32:64 X:32:64 M2 M3 "
HERE = (" rv:0:44 ra:44:90 p:0:90 rv:90:136 ra:136:192 A0 B0 C0 D0 p:90:192 N0 N1 A1 B1 C1 D1 ga:0:30 sa:0:30 x:0:30"
        " ga:42:64 gv:30:42 sa:30:58 m0 m1 x:42:64 x:30:42 sa:58:64 m2 K0 ka1 m3 ka3 K2 n0 n1")
STEPS = ["k:idn k:herd k:nid k:diff k:pc k:za k:tab L:first,gift k:rst k:fill k:ntw k:mid"
         " ev0 GS0 ea1 GS1 GS2 L:dam da0 da1 GD0 GD1 za:0:64 L:s02 E" + DAMS + "L:xv0 +za:0:64" + HERE,
         "GS0 GS1 da0 dv1 GD0 GD1" + DAMS + "L:xv1 +za:0:64" + HERE,
         "GS0 GS1 da0 dv1 GD0 GD1 Sa:0:32 X:0:32 N0 Sa:32:64 X:32:64 N1 L:xv2 ya0 ya1"
         " rv:0:46 ra:46:90 rv:90:136 ra:136:192 p:0:90 A0 B0 C0 D0 ga:0:30 p:90:192 A1 B1 sa:0:30 C1 D1 ga:30:50 x:0:30"
         " m0 sa:30:50 m1 m2 K0 x:30:50 ka1 gv:50:64 sa:50:64 K2 x:50:64 m3 K3"]
VSH = None
PIECES = [[0, 6, 30, 58, 64], [0, 6, 30, 58, 64], [0, 16, 30, 50, 64]]
STEPS = [
 'k:idn k:nid k:herd k:pc k:za k:tab l:first l:gift k:diff l:first l:gift k:rst k:fill k:ntw k:f181 k:fid GS0 ev0 ea1 l:dam l:dam l:dam l:s0 l:s0 l:dam l:s0 iv:10:30 GS1 da1 da0 l:s0 l:dam iv:30:70 GS2 jv:0:30 GD0 l:s0 l:s0 za:0:64 l:xp0 Sa:0:40 Sa:40:64 jv:30:40 E ja:40:70 GD1 X:0:44 M0 M1 l:xp0 l:xp0 X:44:64 rv:0:44 ra:44:90 l:xp0 M3 rv:90:140 ra:140:192 p:0:90 +za:0:64 l:xp0 A0 l:s1 B0 l:s1 l:s1 M2 C0 p:90:192 l:s1 D0 l:s1 N0 l:s1 l:xp1 N1 A1 B1 l:xp1 ga:0:30 C1 sa:0:30 D1 x:0:30 ga:40:64 sa:30:58 gv:30:40 m0 m1 x:52:64 ka1 sv:58:64 m2 x:30:52 K0 K2 m3 ka3 n0 n1',
 'iv:0:16 ia:16:30 GS0 iv:30:52 ia:52:70 GS1 da0 dv1 l:xp1 jv:0:14 ja:14:30 GD0 X:0:42 Sa:0:30 ja:62:70 l:xp1 M0 X:42:64 l:xp1 Sa:30:64 M1 M2 jv:30:62 GD1 k:mid rv:0:44 +za:0:42 ra:44:90 p:0:90 ra:136:192 rv:90:136 p:90:192 l:s2 M3 A0 l:s2 B0 l:s2 C0 l:s2 N1 D0 l:s2 +za:42:64 ga:0:30 l:s2 N0 A1 l:xp2 B1 l:xp2 C1 D1 sa:0:30 ga:40:64 x:0:30 gv:30:40 m0 m1 sv:58:64 x:48:64 sa:30:58 x:30:48 K0 m2 ka1 m3 K2 ka3 n0 n1',
 'iv:0:16 ia:16:30 GS0 iv:30:52 ia:52:70 GS1 da0 dv1 ja:12:30 jv:0:12 GD0 Sa:0:38 X:0:36 X:36:64 l:xp2 l:xp2 Sa:38:64 ja:44:70 N0 l:xp2 N1 ja:30:44 GD1 yv1 rv:0:46 ra:46:92 rv:92:136 ra:136:192 p:0:90 ya0 A0 p:90:192 B0 C0 D0 A1 B1 ga:0:30 C1 D1 sa:0:30 ga:30:50 x:0:30 sa:30:50 sa:50:64 m0 x:30:50 m1 m2 K0 gv:50:64 ka1 K2 m3 x:50:64 K3',
]
CALLS["S1"] = CALLS["S2"] = [(1, 0, True), (1, 1, False), (0, 4, False)]
LOADS = "a:g0 s:h0 a:h1 s:gl a:dl s:rl s:ef"
CHOICE = [[0, 32, 64]] * 3
PIECES = [[0, 18, 32, 56, 64], [0, 18, 32, 56, 64], [0, 16, 32, 50, 64]]
STEPS = [
 'k:idn k:pc k:fill k:nid k:za k:herd k:diff l:first k:f181 l:first k:fid k:rst k:tab k:ntw k:mid GS0 ea0 ea1 l:dam l:dam l:gift l:gift l:dam l:s0 iv:10:30 GS1 l:dam l:s0 l:dam da0 l:s0 da1 iv:30:54 ia:54:70 GS2 za:0:64 jv:0:38 GD0 l:s0 l:s0 ja:38:70 GD1 l:s0 Sv:54:64 l:xp0 Sa:0:54 l:xp0 X:0:52 M1 M0 l:xp0 X:52:64 M3 l:xp0 E M2 +za:0:16 l:xp0 rv:0:24 ra:24:48 p:0:48 rv:48:72 ra:72:96 p:48:96 rv:96:120 ra:120:144 p:96:144 rv:144:168 ra:168:192 p:144:192 A0 N1 N0 B0 +za:16:64 l:s1 l:s1 C0 l:s1 D0 A1 l:s1 B1 ga:0:32 l:s1 sa:0:32 C1 l:s1 D1 ga:52:64 gv:32:52 sa:32:58 x:0:32 x:42:64 m0 m1 sa:58:64 x:32:42 K0 ka1 m2 m3 K2 n0 ka3 n1',
 'iv:0:10 GS0 ia:10:30 GS1 iv:30:58 ia:58:70 GS2 dv1 l:xp1 da0 ja:8:30 l:xp1 jv:0:8 GD0 l:xp1 Sa:0:64 X:0:32 l:xp1 X:32:64 ja:58:70 l:xp1 jv:30:58 GD1 M0 M1 M3 M2 +za:0:42 rv:0:24 ra:24:48 p:0:48 rv:48:72 ra:72:96 p:48:96 rv:96:120 ra:120:144 p:96:144 rv:144:164 ra:164:192 p:144:192 A0 l:s2 B0 l:s2 C0 N0 D0 l:s2 +za:42:64 ga:0:32 A1 l:s2 B1 l:s2 N1 sa:0:32 C1 l:s2 D1 x:0:32 gv:32:44 ga:44:64 sa:32:56 m0 x:38:64 x:32:38 sa:56:64 m1 m2 m3 K0 ka1 n0 ka3 K2 n1',
 'iv:0:10 GS0 ia:10:30 GS1 iv:30:58 ia:58:70 GS2 dv1 l:xp2 l:xp2 da0 Sa:0:32 jv:0:30 GD0 l:xp2 Sa:32:64 X:0:32 N0 l:xp2 X:32:64 N1 ja:30:70 l:xp2 GD1 yv0 rv:0:24 ra:24:48 p:0:48 rv:48:72 ra:72:96 p:48:96 rv:96:120 ra:120:144 p:96:144 rv:144:166 ra:166:192 p:144:192 ya1 A0 B0 C0 D0 ga:0:18 A1 gv:18:32 B1 C1 D1 sa:0:32 ga:32:50 sa:32:50 m0 x:0:32 K0 x:32:50 m1 sa:50:64 m2 ka1 gv:50:64 m3 K2 x:50:64 K3',
]


def split(engs, n):
    parts = [list(engs)]
    while len(parts) < n:
        big = max(len(p) for p in parts)
        i = max(j for j, p in enumerate(parts) if len(p) == big)
        p = parts[i]
        parts[i:i + 1] = [p[:big // 2], p[big // 2:]]
    return parts


def bits(engs):
    m = 0
    for e in engs:
        m |= 1 << e
    return m


def ones(m):
    return bin(m).count("1")


def plan(T, topo, rank):
    n = len(T.cores)
    me = T.cores[rank]
    dests = [(d, T.cores[(rank + 1 + d) % n]) for d in range(n - 1)]
    dests.sort(key=lambda x: not topo.same_plane(me, x[1]))
    handed = set()
    for calls in CALLS.values():
        pos = 0
        for nr, nd, wide in calls:
            handed.update(range(pos, pos + nr))
            pos += nr + nd
    free = sorted((c for c in topo.cores_of(me) if T.rank_of(c) is None), key=lambda c: topo.die(c) == topo.die(me))
    helper = {}
    for i in sorted(handed, reverse=True):
        helper[i] = [h for h in free if topo.may_write(h, dests[i][1])][0]
        free.remove(helper[i])
    off = topo.engines(me, dests[0][1])
    out = {}
    for k, calls in CALLS.items():
        pos, out[k] = 0, []
        for nr, nd, wide in calls:
            c = []
            if nr:
                on = topo.engines(me, helper[pos])
                parts = split(on if wide else [e for e in on if e not in off], nr)
                c += [(pos + i,) + dests[pos + i] + (helper[pos + i], bits(parts[i])) for i in range(nr)]
            if nd:
                parts = split(off, nd)
                c += [(pos + nr + i,) + dests[pos + nr + i] + (None, bits(parts[i])) for i in range(nd)]
            out[k].append(c)
            pos += nr + nd
    return [d for d, c in dests], out


def helper_program(g, core, T, topo):
    for r, c in enumerate(T.cores):
        if core not in topo.cores_of(c):
            continue
        calls, total = plan(T, topo, r)[1], 0
        for k in KEYS:
            for pos, d, dest, h, m in [x for call in calls[k] for x in call if x[3] == core]:
                rid, pid = topo.addr(dest, core)
                win, ar = T[k], T.sem["ar" + k]
                g.wait_ge(ar, ones(m))
                g.remote_dma(win[:, A + SG * d:A + SG * (d + 1)], win[:, 0:SG], ar, T.sem.sentS, pid, rid, topo.mask(core, dest))
                total += ones(topo.mask(core, dest))
        if total:
            g.wait_ge(T.sem.sentS, total)


def rank_program(g, core, T, topo):
    rank = T.rank_of(core)
    if rank is None:
        helper_program(g, core, T, topo)
        return
    OP, AF = AluOpType, ActivationFunctionType
    order, calls = plan(T, topo, rank)
    arrive = {k: 0 for k in KEYS}
    for r in range(len(T.cores)):
        if r != rank:
            for k, cs in plan(T, topo, r)[1].items():
                arrive[k] += sum(ones(m if h is None else topo.mask(h, core))
                                 for call in cs for pos, d, dest, h, m in call if dest == core)

    Q = {"g": g, "pe": g.tensor, "v": g.vector, "a": g.scalar, "s": g.sync}
    cnt = {}
    seen = {q: {} for q in Q}
    clock = {}
    acc = {}

    def wait(q, tok):
        if seen[q].get(tok[0], 0) >= tok[1]:
            return
        Q[q].wait_ge(T.sem[tok[0]], tok[1])
        for s, v in clock.get(tok, {tok[0]: tok[1]}).items():
            if seen[q].get(s, 0) < v:
                seen[q][s] = v

    def bank(n):
        return SCRATCH[n][0] == "psum"

    def note(tok, rd, wr):
        for n, lo, hi in rd + wr:
            if bank(n):
                acc[n] = [e for e in acc.get(n, []) if e[3][0] == tok[0]]
        for n, lo, hi in wr:
            acc[n] = [e for e in acc.get(n, []) if not (lo <= e[0] and e[1] <= hi)] + [(lo, hi, True, tok)]
        for n, lo, hi in rd:
            acc.setdefault(n, []).append((lo, hi, False, tok))

    def op(q, fn, rd, wr, sem=None, inc=1, mark=True):
        need = {}
        for lst, isw in ((rd, False), (wr, True)):
            for n, lo, hi in lst:
                for e in acc.get(n, []):
                    other = bank(n) and e[3][0] != "c_" + q
                    if other or (e[0] < hi and lo < e[1] and (isw or e[2]) and not (q == "pe" and e[3][0] == "c_pe")):
                        need[e[3][0]] = max(need.get(e[3][0], 0), e[3][1])
        for s in sorted(need, key=lambda s: s == "c_" + q):
            wait(q, (s, need[s]))
        ins = fn()
        if not mark:
            return
        s = sem or "c_" + q
        cnt[s] = cnt.get(s, 0) + inc
        if ins is not None:
            ins.then_inc(T.sem[s], inc)
        tok = (s, cnt[s])
        clock[tok] = dict(seen[q])
        clock[tok][s] = cnt[s]
        note(tok, rd, wr)

    def rg(*a):
        return [tuple(a[i:i + 3]) for i in range(0, len(a), 3)]

    V, S = g.vector, g.scalar

    def dma(q, out, in_, rd, wr, sem):
        op(q, lambda: Q[q].dma_start(out, in_), rd, wr, sem=sem, inc=16)

    def mm(b, lo, hi, terms, first=True, last=True):
        rd = [x for t3 in terms for x in t3[2]]

        def fn():
            ins = None
            for i, (l, r, _) in enumerate(terms):
                ins = g.tensor.matmul(T[b][:, lo:hi], l, r, first and i == 0, last and i == len(terms) - 1)
            return ins
        op("pe", fn, rd, rg(b, lo, hi))

    def ts(out, in0, s1, s2, o0, o1, rd, wr):
        if s2 is None:
            op("v", lambda: V.tensor_scalar(out, in0, s1, None, o0), rd, wr)
        else:
            op("v", lambda: V.tensor_scalar(out, in0, s1, s2, o0, o1), rd, wr)

    def tt(out, in0, in1, o, rd, wr):
        op("v", lambda: V.tensor_tensor(out, in0, in1, o), rd, wr)

    def scan(out, d0, d1, o0, rd, wr):
        op("v", lambda: V.tensor_tensor_scan(out, d0, d1, 0.0, o0, OP.max), rd, wr)

    def cp(q, out, in_, rd, wr, add=None, times=None):
        if q == "v":
            if times is not None:
                ts(out, in_, times, 0.0 if add is None else add, OP.mult, OP.add, rd, wr)
            elif add is not None:
                ts(out, in_, add, None, OP.add, None, rd, wr)
            else:
                op("v", lambda: V.tensor_copy(out, in_), rd, wr)
        elif add is None and times is None:
            op("a", lambda: S.activation(out, in_, AF.Copy), rd, wr)
        else:
            op("a", lambda: S.activation(out, in_, AF.Identity, bias=0.0 if add is None else add, scale=times or 1.0), rd, wr)

    def gather(q, dst, d0, win, wn, off, c0, c1, tile=None, add=None, times=None, how=OP.mult):
        if c1 <= c0:
            return
        n = 16 * (c1 - c0)
        src = T[win][:, 0:wn].indirect(T[off][:, c0:c1])
        rd, wr = rg(win, 0, wn, off, c0, c1), rg(dst, d0, d0 + n)
        if tile is None:
            cp(q, T[dst][:, d0:d0 + n], src, rd, wr, add, times)
        else:
            tt(T[dst][:, d0:d0 + n], src, T[tile][:, d0:d0 + n], how, rd + rg(tile, d0, d0 + n), wr)

    def iota(n, w, pattern, base, cm):
        op("g", lambda: g.iota(T[n][:, 0:w], pattern, base, cm, allow_small_or_imprecise_dtypes=True), [], rg(n, 0, w))

    def term(m, n, lo, hi, step=1):
        return (T[m][:], T[n][:, lo:hi:step], rg(m, 0, 128, n, lo, hi))

    for k in KEYS:
        note(("ar" + k, arrive[k]), [], rg(k, A, W))

    loads = {"h0": (T.hap[:, 0:1024], T.haps[:, 0:1024], rg("hap", 0, 1024)), "h1": (T.hap[:, 1024:2048], T.haps[:, 1024:2048], rg("hap", 1024, 2048)),
             "gl": (T.gl[:], T.gift[:], rg("gl", 0, 210)), "rl": (T.rl[:], T.rival[:], rg("rl", 0, 576)),
             "g0": (T.g0[:, 0:10], T.gift[:, 10 * order[0]:10 * order[0] + 10], rg("g0", 0, 10)),
             "dl": (T.dl[:], T.dam[:], rg("dl", 0, 192)), "ef": (T.ef[:, 0:1], T.eff[:], rg("ef", 0, 1))}
    for w in LOADS.split():
        q, n = w.split(":")
        dma(q, loads[n][0], loads[n][1], [], loads[n][2], "l_" + n)
    iota("iot", 128, [[1, 128]], 0, -1)
    op("g", lambda: g.iota(T.pc[:, 0:1], [[1, 1]], 0, 1), [], rg("pc", 0, 1))
    iota("zz", 96, [[0, 3], [2, 32]], -17, -2)
    iota("kk", 192, [[0, 64], [-1, 3]], 2, 0)
    iota("jb", 8, [[32, 8]], 0, 0)
    iota("cid", 192, [[217, 3], [1200, 64]], 0, 75)
    iota("cir", 576, [[217, 3], [1200, 64], [0, 3]], 389, 75)

    def diag(n, lo, at, x, rd=()):
        ts(T[n][:, lo:lo + 128], T.iot[:], at, x, OP.is_equal, OP.mult, rg("iot", 0, 128, *rd), rg(n, lo, lo + 128))

    def col(c, src, x, y):
        ts(T.cols[:, c:c + 1], T.pc[:, src:src + 1], x, y, OP.mult, OP.add, rg("pc", src, src + 1), rg("cols", c, c + 1))

    def constant(n):
        if n in DIAG:
            diag(n, 0, 0.0, DIAG[n])
        elif n == "fill":
            op("v", lambda: V.memset(T.bm[:], 0.0), [], rg("bm", 0, 144))
        elif n == "mid":
            op("v", lambda: V.memset(T.mid[:], 127.5), [], rg("mid", 0, 512))
        elif n == "pc":
            ts(T.pc[:, 1:2], T.pc[:, 0:1], 112, None, OP.bitwise_and, None, rg("pc", 0, 1), rg("pc", 1, 2))
            col(0, 1, 2.0, 0.0)
            col(1, 1, -75.0, 0.0)
        elif n == "odd":
            ts(T.pc[:, 2:3], T.pc[:, 0:1], 1, None, OP.bitwise_and, None, rg("pc", 0, 1), rg("pc", 2, 3))
            col(3, 2, 64.0, -32.0)
        elif n == "abs":
            op("a", lambda: S.activation(T.off[:], T.iot[:], AF.Abs), rg("iot", 0, 128), rg("off", 0, 128))
            op("a", lambda: S.activation(T.far[:], T.iot[:], AF.Abs, bias=T.cols[:, 3:4], scale=64.0), rg("iot", 0, 128, "cols", 3, 4), rg("far", 0, 128))
        elif n == "za":
            op("a", lambda: S.activation(T.za[:], T.zz[:], AF.Abs, bias=T.cols[:, 0:1]), rg("zz", 0, 96, "cols", 0, 1), rg("za", 0, 96))
        elif n == "far":
            tt(T.far[:], T.far[:], T.off[:], OP.add, rg("far", 0, 128, "off", 0, 128), rg("far", 0, 128))
            ts(T.off[:], T.far[:], -1.0, 33.5, OP.mult, OP.add, rg("far", 0, 128), rg("off", 0, 128))
        elif n[:2] == "fw":
            for r in range(4 * int(n[3]), 4 * int(n[3]) + 4):
                if n[2] == "a":
                    op("a", lambda: S.activation(T.fw[:, :, r], T.off[:], AF.Relu, bias=float(r)), rg("off", 0, 128), rg("fw", r, r + 1))
                else:
                    ts(T.fw[:, :, r], T.off[:], float(r), 0.0, OP.add, OP.max, rg("off", 0, 128), rg("fw", r, r + 1))
        elif n == "mix":
            for c, x, y in ((4, -1.0, 1.0), (5, 1.0, 0.0), (6, 1.0, -1.0), (7, -1.0, 0.0)):
                col(c, 2, x, y)
            for i, at in enumerate((0.0, 0.0, 1.0, -1.0)):
                diag("mix", 128 * i, at, T.cols[:, 4 + i:5 + i], ("cols", 4 + i, 5 + i))
        elif n == "rst":
            ts(T.rst[:], T.kk[:, 0:144], 2.0, -4194304.0, OP.is_equal, OP.mult, rg("kk", 0, 144), rg("rst", 0, 144))
            ts(T[KC[0]][:, KC[1]:KC[2]], T.kk[:], 32.0, None, OP.mult, None, rg("kk", 0, 192), rg(*KC))
            ts(T.rst[:], T.rst[:], 0.25, None, OP.add, None, rg("rst", 0, 144), rg("rst", 0, 144))
        elif n == "tbd":
            ts(T.tbd[:], T.za[:, 0:32], 16.0, -2.0, OP.is_ge, OP.mult, rg("za", 0, 96), rg("tbd", 0, 32))
        elif n == "tab":
            ts(T.tab[:], T.za[:], 16.0, 0.5, OP.is_ge, OP.subtract, rg("za", 0, 96), rg("tab", 0, 96))
        elif n == "herd":
            for h in range(2):
                mm("ps%d" % h, 0, 512, [term("idn", "hap", 1024 * h, 1024 * (h + 1), 2), term("idn", "hap", 1024 * h + 1, 1024 * (h + 1), 2)])
        elif n == "diff":
            for h in range(2):
                mm("pw%d" % h, 0, 512, [term("idn", "hap", 1024 * h + 1, 1024 * (h + 1), 2), term("nid", "hap", 1024 * h, 1024 * (h + 1), 2)])

    runs = []
    for d in order:
        if runs and d > runs[-1][-1] and (len(runs[-1]) == 1 or d - runs[-1][-1] == runs[-1][1] - runs[-1][0]):
            runs[-1].append(d)
        else:
            runs.append([d])
    starts = [sum(len(r) for r in runs[:i]) for i in range(len(runs) + 1)]

    def gift_lists():
        for run, pos in zip(runs, starts):
            lo, hi, step = 10 * G * pos, 10 * G * (pos + len(run)), run[1] - run[0] if len(run) > 1 else 1
            cp("v", T.goff[:, lo:hi], T.gl[:, :, run[0]:run[-1] + 1:step, :], rg("gl", 0, 210), rg("goff", lo, hi))
            yield

    def first_lists():
        for pos, d, dest, h, m in calls["S0"][0]:
            lo, hi = 10 * pos, 10 * (pos + 1)
            for n, s in (("gev", 0.0), ("god", 1.0)):
                if "g0" in LOADS:
                    ts(T[n][:, lo:hi], T.g0[:, 0:10], 2.0, s, OP.mult, OP.add, rg("g0", 0, 10), rg(n, lo, hi))
                else:
                    ts(T[n][:, lo:hi], T.gl[:, 0, d, :], 2.0, s, OP.mult, OP.add, rg("gl", 0, 210), rg(n, lo, hi))
                yield

    def first_sums(lo, hi):
        for a in range(lo, hi, 20):
            b = min(a + 20, hi)
            op("a", lambda: S.activation(T.R[:, 16 * a:16 * b], T.hap[:].indirect(T.gev[:, a:b]), AF.Identity, bias=-255.0),
               rg("hap", 0, 2048, "gev", a, b), rg("R", 16 * a, 16 * b))
            tt(T.gS[:, 16 * a:16 * b], T.hap[:].indirect(T.god[:, a:b]), T.R[:, 16 * a:16 * b], OP.add,
               rg("hap", 0, 2048, "god", a, b, "R", 16 * a, 16 * b), rg("gS", 16 * a, 16 * b))

    def gift_gather(e, buf, win, t, lo, hi):
        for i, run in enumerate(runs):
            a, b = max(lo, 10 * starts[i]), min(hi, 10 * starts[i + 1])
            o = 10 * (G - 1) * starts[i] + 10 * t * len(run)
            gather(e, buf, 16 * a, win, A, "goff", o + a, o + b)

    def gifts(k, t, ci):
        win, sent = "%s%d" % (k, t), "sent" + k
        bufs = ["gS", "gD"] if CHAIN and k == "D" else ["g" + k]
        call, ar = calls[win][ci], T.sem["ar" + win]
        lo, hi = 10 * call[0][0], 10 * (call[-1][0] + 1)
        if win == "S0" and ci == 0:
            first_sums(lo, hi)
        elif VSH:
            mid = lo + 2 * int(round((hi - lo) * VSH[win] / 2))
            gift_gather("v", "g" + k, win, t, lo, mid)
            gift_gather("a", "g" + k, win, t, mid, hi)
        tr = []
        for pos, d, dest, h, m in call:
            rid, pid = topo.addr(dest if h is None else h, core)
            at = A + SG * d if h is None else 0
            tr.append(RemoteDMATransfer(dst_ids=[DstId(rid=rid, pnc=pid)], dma_engine_mask=m, remote_sem=ar,
                                        srcs=[T[b][:, SG * pos:SG * (pos + 1)] for b in bufs], dsts=[T[win][:, at:at + SG]],
                                        alu_op=len(bufs) - 1))

        def fn():
            g.remote_dma_fused(tr, local_sem=T.sem[sent])
        if ci + 1 < len(calls[win]):
            op("g", fn, [(b, 16 * lo, 16 * hi) for b in bufs], [], mark=False)
        else:
            op("g", fn, [(b, 0, 1120) for b in bufs], [], sem=sent, inc=sum(ones(x[4]) for c in calls[win] for x in c))

    def cross(src, ci, ti, lo, hi, q="v"):
        n = hi - lo
        if q == "p":
            mm("pv0", 320, 512, [term("f181", src, lo, hi), term("fid", ci, lo, hi)])
            yield
            ts(T[ti][:, lo:hi], T.pv0[:, 320:512], T.cols[:, 1:2], None, OP.add, None, rg("pv0", 320, 512, "cols", 1, 2), rg(ti, lo, hi))
            yield
            return
        cp(q, T.pv1[:, 0:n], T[src][:, lo:hi], rg(src, lo, hi, "cols", 1, 2), rg("pv1", 0, n), add=T.cols[:, 1:2], times=181.0)
        yield
        tt(T[ti][:, lo:hi], T.pv1[:, 0:n], T[ci][:, lo:hi], OP.add, rg("pv1", 0, n, ci, lo, hi), rg(ti, lo, hi))
        yield

    def field(out, src, shift, mask, lo, hi):
        ts(T[out][:, lo:hi], T[src][:, lo:hi], shift, mask, OP.logical_shift_right, OP.bitwise_and, rg(src, lo, hi), rg(out, lo, hi))

    def dam_lists():
        steps = cross("dl", "cid", "di", 0, 192)
        next(steps)
        yield
        cp("v", T.doff[:], T.dl[:], rg("dl", 0, 192), rg("doff", 0, 192))
        yield
        yield from steps
        if not RAMP:
            field("dc", "di", 5, 31, 0, 192)
            yield
            cp("v", T.dz[:], T.dc[:], rg("dc", 0, 192), rg("dz", 0, 192))
            yield
            return
        field("ds", "di", 9, 1, 0, 192)
        field("dc", "di", 5, 15, 0, 192)
        sg = T.pv1[:, 0:192]
        ts(sg, T.ds[:], -1024.0, 512.0, OP.mult, OP.add, rg("ds", 0, 192), rg("pv1", 0, 192))
        yield
        tt(T.wl[:, 0:192], T.dc[:], sg, OP.mult, rg("dc", 0, 192, "pv1", 0, 192), rg("wl", 0, 192))
        yield
        tt(T.wl[:, 192:384], T.wl[:, 0:192], sg, OP.add, rg("wl", 0, 192, "pv1", 0, 192), rg("wl", 192, 384))
        yield

    def sort_rivals(t0, t1):
        a, b, c = (T.rl[:, t0:t1, k, :] for k in range(3))
        n, o, e = 64 * (t1 - t0), 192 * t0, 192 * t1
        p = 320 if n == 64 else 0
        rh, rl = rg("pv0", p, p + n), rg("pv0", p + n, p + 2 * n)
        rr, hi, lo, tb = rg("rl", 0, 576), T.pv0[:, p:p + n], T.pv0[:, p + n:p + 2 * n], T.tb[:, 0:n]
        tt(hi, a, b, OP.max, rr, rh)
        yield
        tt(lo, a, b, OP.min, rr, rl)
        yield
        tt(tb, hi, c, OP.min, rr + rh, rg("tb", 0, 192))
        yield
        tt(T.rs[:, o:e:3], hi, c, OP.max, rr + rh, rg("rs", o, o + 1))
        yield
        tt(T.rs[:, o + 2:e:3], lo, c, OP.min, rr + rl, rg("rs", o + 2, o + 3))
        yield
        tt(T.rs[:, o + 1:e:3], lo, tb, OP.max, rl + rg("tb", 0, 192), rg("rs", o + 1, o + 2, "rs", o + 3, e))
        yield

    def rival_lists(t, q):
        o, e = 192 * t, 192 * (t + 1)
        steps = cross("rs", "cir", "ti", o, e, q)
        next(steps)
        yield
        cp("v", T.roff[:, o:e], T.rs[:, o:e], rg("rs", o, e), rg("roff", o, e))
        yield
        yield from steps
        field("tj", "ti", 5, 31, o, e)
        yield
        tt(T.u2[:, o:e], T.tj[:, o:e], T[KC[0]][:, KC[1]:KC[2]], OP.add, rg("tj", o, e, *KC), rg("u2", o, e))
        yield

    def weave(*gens):
        gens = list(gens)
        while gens:
            gens = [x for x in gens if next(x, 1) is None]

    def values(b, base, c0, c1):
        mm(b, c0 - base, c1 - base, [(T.bm[:, 15 - q:143 - q], T.R[:, 16 * c0 + q:16 * c1:16], rg("bm", 0, 144, "R", 16 * c0, 16 * c1))
                                     for q in range(16)])

    def ramp(b, t, par):
        o = 192 * par + 64 * t

        def fn():
            for q in range(par, 16, 2):
                ins = g.tensor.matmul(T[b][:, q // 2:512:8], T.fw[:, q:128:16, :], T.wm[:, o:o + 64], True, True)
            return ins
        op("pe", fn, rg("fw", 0, 16, "wm", o, o + 64), rg(b, 0, 512))

    def choose(t, h, part):
        c0, c1 = CHOICE[t][h:h + 2]
        b, lo, hi, n = "pv%d" % (h % 2), 3 * c0, 3 * c1, 3 * (c1 - c0)
        pv, M, nf = T[b][:, 0:n], T.M[:, lo:hi], T.nf[:, lo:hi]
        if part == "A":
            scan(M, T.rst[:, 0:n], pv, OP.add, rg("rst", 0, n, b, 0, n), rg("M", lo, hi))
        elif part == "B":
            tt(nf, pv, M, OP.not_equal, rg(b, 0, n, "M", lo, hi), rg("nf", lo, hi))
        elif part == "C":
            for src, e in (("u2", 2 * lo + n), ("rs", 2 * lo)):
                scan(T.sel[:, e:e + n], nf, T[src][:, 192 * t + lo:192 * t + hi], OP.mult, rg("nf", lo, hi, src, 192 * t, 192 * t + 192), rg("sel", e, e + n))
        else:
            cp("v", T.so[:, 2 * c0:2 * c1], T.sel[:, 2 * lo + 2:2 * hi:3], rg("sel", 2 * lo, 2 * hi), rg("so", 2 * c0, 2 * c1))

    running = {}
    XW = ("hid", "nid") if RAMP else ("idn", "ntw")

    def step(t, w):
        Sw, Dw, nS, nD, last = "S%d" % t, "D%d" % t, "S%d" % (t + 1), "D%d" % (t + 1), t == G - 1
        nN = "Nd" if last else nD
        if w[0] in "Ll":
            lists = {"gift": gift_lists, "dam": dam_lists, "first": first_lists}
            for x in w[2:].split(","):
                if x not in running:
                    running[x] = lists[x]() if x in lists else sort_rivals(int(x[1]), int(x[-1]) + 1) if x[0] == "s" else rival_lists(int(x[2]), x[1])
            if w[0] == "L":
                weave(*[running[x] for x in w[2:].split(",")])
            else:
                next(running[w[2:]], 1)
        elif w[:2] == "k:":
            for x in w[2:].split(","):
                constant(x)
        elif w == "E":
            cp("v", T.cols[:, 2:3], T.ef[:, 0:1], rg("ef", 0, 1), rg("cols", 2, 3))
            ts(T.bm[:, 15:143:16], T.jb[:], T.cols[:, 0:1], T.cols[:, 2:3], OP.is_equal, OP.mult,
               rg("jb", 0, 8, "cols", 0, 3), rg("bm", 0, 144))
        elif w[:3] == "mix":
            for h in range(2):
                mm("ps3", 192 * h, 192 * (h + 1), [(T.mix[:, 128 * (h + 2 * i):128 * (h + 2 * i + 1)], T.wl[:, 192 * i:192 * (i + 1)],
                                                    rg("mix", 0, 512, "wl", 0, 384)) for i in range(2)])
            cp(w[3], T.wm[:, 0:384], T.ps3[:, 0:384], rg("ps3", 0, 384), rg("wm", 0, 384))
        elif w[:3] == "ADD":
            to, src = (Dw, Sw) if w[3] == "S" else (nD, "Xd")
            op("g", lambda: g.dma_start(T[to][:, 0:A], T[src][:, 0:A], accum_op=OP.add), rg(src, 0, A, to, 0, A), rg(to, 0, A), sem="add" + w[3], inc=16)
        elif w[0] == "G":
            gifts(w[1], t, int(w[2]))
        elif w[0] in "ABCD":
            choose(t, int(w[1]), w[0])
        elif ":" in w:
            e, c0, c1 = w.split(":")
            c0, c1 = int(c0), int(c1)
            if e == "p":
                h = max(i for i, c in enumerate(CHOICE[t]) if 3 * c <= c0)
                values("pv%d" % (h % 2), 3 * CHOICE[t][h], c0, c1)
            elif e[0] == "r":
                gather(e[1], "R", 16 * c0, Sw, W, "roff", 192 * t + c0, 192 * t + c1)
            elif e[0] in "ij":
                k = "SD"[e[0] == "j"]
                gift_gather(e[1], "g" + k, k + str(t), t, c0, c1)
            elif e[0] == "S":
                gather(e[1], "Sd", 16 * c0, Sw, A, "doff", 64 * t + c0, 64 * t + c1, times=0.5)
            elif e[0] == "a":
                gather(e[1], nN, 16 * c0, Dw, A, "doff", 64 * t + c0, 64 * t + c1)
            elif e[0] == "c":
                gather("v", "Sd", 16 * c0, Sw, A, "doff", 64 * t + c0, 64 * t + c1, tile=nN, how=OP.add)
            elif e[0] == "b":
                gather("v", "Xd", 16 * c0, "tbd", 32, "dz", 64 * t + c0, 64 * t + c1, tile="Sd")
            elif e[0] == "X":
                gather("v", "Xd", 16 * c0, Dw, A, "doff", 64 * t + c0, 64 * t + c1, tile="sgd%d" % t)
            elif e[0] == "z":
                gather(e[1], "sgd%d" % t, 16 * c0, "tab", 96, "dz", 64 * t + c0, 64 * t + c1)
            else:
                h = max(i for i, c in enumerate(CHOICE[t]) if c <= c0)
                p, z = CHOICE[t][h:h + 2]
                if e[0] == "g":
                    gather(e[1], "sgs", 16 * c0, "tab", 96, "so", z + c0, z + c1)
                elif e[0] == "s":
                    gather(e[1], "Ss", 16 * c0, Sw, W, "so", p + c0, p + c1, times=0.5)
                else:
                    gather("v", "Xs", 16 * c0, Dw, W, "so", p + c0, p + c1, tile="sgs")
        elif w[0] in "deWYNnyH":
            h = int(w[-1])
            lo, hi, b, rb = 512 * h, 512 * (h + 1), "pw%d" % h, RBANK[t] + str(h + 2 * (RBANK[t] == "ps"))
            if w[0] == "d":
                cp(w[1], T[Dw][:, lo:hi], T[b][:], rg(b, 0, 512), rg(Dw, lo, hi))
            elif w[0] == "e":
                cp(w[1], T.S0[:, lo:hi], T["ps%d" % h][:], rg("ps%d" % h, 0, 512), rg("S0", lo, hi), add=-255.0)
            elif w[0] == "W":
                ramp(rb, t, h)
            elif w[0] == "Y":
                op("a", lambda: S.activation(T["sgd%d" % t][:, h:A:2], T[rb][:], AF.Sign, scale=-1.0), rg(rb, 0, 512), rg("sgd%d" % t, h, A if h else 1))
            elif w[0] == "H":
                cp(w[1], T.D0[:, lo:hi], T.hap[:, 2 * lo:2 * hi:2], rg("hap", 2 * lo, 2 * hi), rg("D0", lo, hi), add=255.0, times=-2.0)
            elif w[0] == "N" and CHAIN:
                mm(b, 0, 512, [term("nhd", nN, lo, hi), term("nhd", "Xd", lo, hi)])
            elif w[0] == "N":
                mm(b, 0, 512, [term("idn" if last else "ntw", "Sd", lo, hi), term(XW[0] if last else XW[1], "Xd", lo, hi)], last=last)
            elif w[0] == "n":
                mm(b, 0, 512, [term("idn", nS, lo, hi)], first=False)
            else:
                cp(w[1], T.hap[:, 2 * lo:2 * hi:2], T[b][:], rg(b, 0, 512), rg("hap", 2 * lo, 2 * hi), add=127.5)
        else:
            q = int(w[-1])
            lo, hi, b = 16 * PIECES[t][q], 16 * PIECES[t][q + 1], "ps%d" % q
            n = hi - lo
            out, wr = (T.hap[:, 2 * lo + 1:2 * hi:2], rg("hap", 2 * lo, 2 * hi)) if last else (T[nS][:, lo:hi], rg(nS, lo, hi))
            if w[0] == "M" and CHAIN:
                mm(b, 0, n, [term("nhd", nN, lo, hi), term("nhd", "Xd", lo, hi)], last=False)
            elif w[0] == "M":
                mm(b, 0, n, [term("idn", "Sd", lo, hi), term(XW[0], "Xd", lo, hi)], last=False)
            elif w[0] == "m":
                if "K%d" % q not in STEPS[t]:
                    mm(b, 0, n, [term("idn", "Ss", lo, hi), term("idn", "Xs", lo, hi)], first=last)
                else:
                    mm(b, 0, n, ([term("idn", "mid", 0, n)] if last else []) + [term("idn", "Ss", lo, hi)], first=last)
            else:
                if w[0] == "K":
                    tt(out, T[b][:, 0:n], T.Xs[:, lo:hi], OP.add, rg(b, 0, n, "Xs", lo, hi), wr)
                else:
                    cp(w[1], out, T[b][:, 0:n], rg(b, 0, n), wr, add=127.5 if last else None)
                if last:
                    dma("s", T.y[:, 2 * lo:2 * hi], T.hap[:, 2 * lo:2 * hi], wr, [], "st")

    for t in range(G):
        for w in STEPS[t].split():
            step(t + (w[0] == "+") - (w[0] == "-"), w.lstrip("+-"))

    for s in sorted(cnt, key=lambda s: s == "st"):
        wait("g", (s, cnt[s]))
